import numpy as np
import ml_dtypes


def mxq(x, axis, fmt="e4m3"):
    dtype, down = {"e4m3": (ml_dtypes.float8_e4m3fn, 7), "e5m2": (ml_dtypes.float8_e5m2, 14)}[fmt]
    v = np.moveaxis(np.asarray(x, np.float32).astype(ml_dtypes.bfloat16).astype(np.float64), axis, -1)
    blocks = v.reshape(v.shape[:-1] + (-1, 32))
    amax = np.abs(blocks).max(-1, keepdims=True)
    byte = np.maximum(np.where(amax > 0, np.frexp(amax)[1] - 1 + 127, 0) - down, 1)
    scale = np.exp2(byte - 127.0)
    codes = (blocks / scale).astype(np.float32).astype(dtype).astype(np.float64)
    return np.moveaxis((codes * scale).reshape(v.shape), -1, axis)


WIDE = False


def mx_kscale(k):
    if not WIDE:
        return np.ones(k)
    levels = np.array([30, -30])
    if k % 512:
        return np.exp2(np.random.permutation(np.resize(levels, k // 32))).repeat(32)
    a = np.empty((k // 512, 16))
    for p in range(k // 512):
        a[p, :8] = np.random.permutation(np.resize(levels, 8))
        for g in range(8):
            far = levels[np.abs(levels - a[p, g]) >= 10]
            a[p, g + 8] = far[np.random.randint(len(far))]
    return np.exp2(a.ravel()).repeat(32)


BF16 = ml_dtypes.bfloat16


def bf(x):
    return np.asarray(x, np.float32).astype(BF16)


def f64(x):
    return np.asarray(x).astype(np.float64)


M, K, N, P, S, D, C = 2048, 512, 1024, 512, 384, 64, 4


def setup_inputs():
    s, t = mx_kscale(K), mx_kscale(N)
    return {"fine": bf(np.random.standard_normal((M, K)) * s),
            "coarse": bf(np.random.standard_normal((M // C, K)) * s),
            "lod": bf(np.random.uniform(0.0, 1.0, M)),
            "w_win": bf(np.random.standard_normal((K, N)) / np.sqrt(K) / s[:, None]),
            "center": bf(0.4 * np.random.standard_normal(N)),
            "width": bf(1 + 0.1 * np.random.standard_normal(N)),
            "w_car": bf(np.random.standard_normal((K, N)) / np.sqrt(K) / s[:, None] * t),
            "b_car": bf(0.4 * np.random.standard_normal(N) * t),
            "w_out": bf(2 * np.random.standard_normal((N, P)) / np.sqrt(N) / t[:, None]),
            "b_out": bf(0.4 * np.random.standard_normal(P))}


def reference(fine, coarse, lod, w_win, center, width, w_car, b_car, w_out, b_out):
    l = f64(lod).reshape(M // C, C, 1)
    x = ((1 - l) * f64(fine).reshape(M // C, C, K) + l * f64(coarse)[:, None, :]).reshape(M, K)
    xq = mxq(x, 1, "e4m3")
    a = xq @ mxq(f64(w_win), 0, "e4m3")
    v = (xq @ mxq(f64(w_car), 0, "e4m3")) + f64(b_car)
    z = f64(width) * (a + f64(center))
    h = np.exp(-0.5 * z * z) * v
    y = (mxq(h, 1, "e5m2") @ mxq(f64(w_out), 0, "e4m3")) + f64(b_out)
    material = np.tanh(y[:, :S])
    p, q = y[:, S:S + D], y[:, S + D:]
    r = 1 / np.sqrt(1 + p * p + q * q)
    normal = np.concatenate([p * r, q * r, r], axis=1)
    return material, normal

@@ -1,0 +1,453 @@
+from contextlib import ExitStack
+
+import concourse.mybir as mybir
+from concourse.masks import make_identity
+
+M, K, N, PO, S, D = 2048, 512, 1024, 512, 384, 64
+FLOPS = 2 * M * K * N * 2 + 2 * M * N * PO
+
+F32 = mybir.dt.float32
+BF16 = mybir.dt.bfloat16
+U32 = mybir.dt.uint32
+U8 = mybir.dt.uint8
+E4 = mybir.dt.float8_e4m3fn_x4
+E5 = mybir.dt.float8_e5m2_x4
+ALU = mybir.AluOpType
+ACT = mybir.ActivationFunctionType
+
+P = 128
+GROUPS = 4
+CHUNKS = [(0, 0, 4), (1, 0, 4), (2, 0, 4), (3, 0, 2), (3, 2, 2)]
+D_ENG = "GGGGGGGGGV"
+D_G = [320, 320, 512, 512, 512, 352, 256, 256, 256, 0]
+F_ENG = "VVVVVVVVVVVVVVVV"
+H_ENG = "VVSSSSSS"
+M_ENG = "SSSSSVVVVSSV"
+SQ_ENG = "SSVVVVVV"
+SUM_ENG = "VVVVVVVV"
+MUL_ENG = "VVVV"
+BLEND_AT = {4: 0, 5: 1, 6: 3, 7: 4}
+A_BUFS = 3
+V_BUFS = 2
+Y_BUFS = 2
+
+
+def tile_windowed_texture_decoder_f3_kernel(
+    tc, fine, coarse, lod, w_win, center, width, w_car, b_car, w_out, b_out, material, normal
+):
+    nc = tc.nc
+    with ExitStack() as ctx:
+        keep = ctx.enter_context(tc.tile_pool(name="keep", bufs=1))
+        work = ctx.enter_context(tc.tile_pool(name="work", bufs=2))
+        psum = ctx.enter_context(tc.psum_pool(name="psum", bufs=1))
+        ctx.enter_context(tc.manual_schedule())
+
+        fine_v = fine.rearrange("(p g c) k -> p g c k", g=GROUPS, c=4)
+        coarse_v = coarse.rearrange("(p g) k -> p g k", g=GROUPS)
+        material_v = material.rearrange("(p r) s -> p r s", r=16)
+        normal_v = normal.rearrange("(p r) s -> p r s", r=16)
+
+        lod_sb = keep.tile([P, 16], BF16, name="lod_sb")
+        nc.sync.dma_start(out=lod_sb[:], in_=lod.rearrange("(p r) -> p r", r=16))
+        coarse_sb = {}
+        fine_sb = {}
+        w_raw = {}
+
+        def load_coarse(g):
+            coarse_sb[g] = keep.tile([P, K], BF16, name="coarse%d" % g)
+            nc.sync.dma_start(out=coarse_sb[g][:], in_=coarse_v[:, g, :])
+
+        def load_fine(g, half):
+            fine_sb[g, half] = keep.tile([P, 2, K], BF16, name="fine%d_%d" % (g, half))
+            nc.sync.dma_start(out=fine_sb[g, half][:], in_=fine_v[:, g, 2 * half : 2 * half + 2, :])
+
+        def load_w(which, hh, half):
+            t = keep.tile([P, 4, 256], BF16, name="raw_%s%d_%d" % (which, hh, half))
+            w_raw[which, hh, half] = t
+            if which == "out":
+                src = w_out[512 * hh : 512 * hh + 512, 256 * half : 256 * half + 256]
+            else:
+                c0 = 512 * hh + 256 * half
+                src = (w_win if which == "win" else w_car)[:, c0 : c0 + 256]
+            nc.sync.dma_start(out=t[:], in_=src.rearrange("(p j) n -> p j n", j=4))
+
+        def load_channel_vector(vec, name):
+            t = keep.tile([P, 2, 4], BF16, name=name)
+            nc.gpsimd.dma_start(out=t[:], in_=vec.rearrange("(h p t) -> p h t", h=2, t=4))
+            return t[:].rearrange("p h t -> p (h t)")
+
+        load_coarse(0)
+        load_w("win", 0, 0)
+        load_fine(0, 0)
+        load_w("win", 0, 1)
+        load_fine(0, 1)
+        load_w("car", 0, 0)
+        load_w("car", 0, 1)
+        load_coarse(1)
+        load_fine(1, 0)
+        load_w("win", 1, 0)
+        load_w("win", 1, 1)
+        load_fine(1, 1)
+        for which, hh in (("car", 1), ("out", 0), ("out", 1)):
+            load_w(which, hh, 0)
+            load_w(which, hh, 1)
+        bias_out = keep.tile([P, PO], BF16, name="bias_out")
+        nc.sync.dma_start(out=bias_out[:], in_=b_out.partition_broadcast(P))
+        for g in (2, 3):
+            load_coarse(g)
+            load_fine(g, 0)
+            load_fine(g, 1)
+
+        width_bf = load_channel_vector(width, "width_bf")
+        center_bf = load_channel_vector(center, "center_bf")
+        bias_car = load_channel_vector(b_car, "bias_car")
+        ident = keep.tile([P, P], F32, name="ident")
+        make_identity(nc, ident[:])
+        warm = keep.tile([P, 1], F32, name="warm")
+        warm_out = keep.tile([P, 1], F32, name="warm_out")
+        nc.vector.memset(warm[:], 0.0)
+        nc.scalar.activation(out=warm_out[:], in_=warm[:], func=ACT.Exp)
+        win_scale = keep.tile([P, 8], F32, name="win_scale")
+        win_bias = keep.tile([P, 8], F32, name="win_bias")
+        nc.gpsimd.tensor_copy(out=win_scale[:], in_=width_bf)
+        nc.gpsimd.tensor_tensor(out=win_bias[:], in0=width_bf, in1=center_bf, op=ALU.mult)
+        lod_f = keep.tile([P, 16], F32, name="lod_f")
+        fine_share = keep.tile([P, 16], F32, name="fine_share")
+        nc.vector.tensor_copy(out=lod_f[:], in_=lod_sb[:])
+        nc.vector.tensor_scalar(out=fine_share[:], in0=lod_sb[:], scalar1=-1.0, scalar2=1.0, op0=ALU.mult, op1=ALU.add)
+
+        def interleave(eng, dst, src, permute):
+            if eng == "G":
+                if permute:
+                    o = dst
+                    i = src.rearrange("p j (m t) -> p t m j", t=4)
+                else:
+                    o = dst
+                    i = src.rearrange("p j n -> p n j")
+                nc.gpsimd.tensor_scalar(out=o, in0=i, scalar1=1.0, scalar2=0.0, op0=ALU.mult, op1=ALU.add)
+                return
+            if permute:
+                o = dst.rearrange("p t (m i) j -> p m t i j", i=2)
+                i = src.rearrange("p j (m i t) -> p m t i j", i=2, t=4)
+            else:
+                o = dst.rearrange("p (c i) j -> p c j i", i=4)
+                i = src.rearrange("p j (c i) -> p c j i", i=4)
+            if eng == "V":
+                nc.vector.tensor_copy(out=o, in_=i)
+            else:
+                nc.scalar.copy(out=o, in_=i)
+
+        w_order = [("win", 0), ("car", 0), ("win", 1), ("car", 1), ("out", 0), ("out", 1)]
+        w_grouped, w_codes, w_scales = {}, {}, {}
+
+        def w_interleave(n, half):
+            key = w_order[n]
+            if half == 0:
+                w_grouped[key] = work.tile([P, 2048], BF16, name="wg%d" % n, tag="w_grouped", bufs=3, align_bytes=64)
+            if key[0] == "out":
+                dst = w_grouped[key][:].rearrange("p (n j) -> p n j", j=4)[:, 256 * half : 256 * half + 256, :]
+            else:
+                dst = w_grouped[key][:].rearrange("p (t m j) -> p t m j", t=4, j=4)[:, :, 64 * half : 64 * half + 64, :]
+            interleave(M_ENG[2 * n + half], dst, w_raw[key + (half,)][:], key[0] != "out")
+
+        def w_quantize(n):
+            key = w_order[n]
+            w_codes[key] = keep.tile([P, 512], U32, name="wc%d" % n, align_bytes=64)
+            w_scales[key] = keep.tile([P, 512], U8, name="ws%d" % n, align_bytes=64)
+            nc.vector.quantize_mx(out=w_codes[key][:].bitcast(E4), scales=w_scales[key][:], in_=w_grouped[key][:])
+
+        coarse_part, x_bf, x_grouped, x_codes, x_scales = {}, {}, {}, {}, {}
+
+        def x_coarse(r):
+            g = r // 4
+            t = work.tile([P, K], F32, name="cp%d" % r, tag="coarse_part", bufs=4)
+            coarse_part[r] = t
+            if F_ENG[r] == "V":
+                nc.vector.tensor_scalar(out=t[:], in0=coarse_sb[g][:], scalar1=lod_f[:, r : r + 1], scalar2=None, op0=ALU.mult)
+            elif F_ENG[r] == "G":
+                nc.gpsimd.tensor_scalar(out=t[:], in0=coarse_sb[g][:], scalar1=lod_f[:, r : r + 1], scalar2=0.0, op0=ALU.mult, op1=ALU.add)
+            else:
+                nc.scalar.activation(out=t[:], in_=coarse_sb[g][:], func=ACT.Copy, scale=lod_f[:, r : r + 1])
+
+        def x_blend(r):
+            g, c = divmod(r, 4)
+            x_bf[r] = work.tile([P, K], BF16, name="xb%d" % r, tag="x_bf", bufs=4)
+            nc.vector.scalar_tensor_tensor(
+                out=x_bf[r][:], in0=fine_sb[g, c // 2][:, c % 2, :], scalar=fine_share[:, r : r + 1],
+                in1=coarse_part[r][:], op0=ALU.mult, op1=ALU.add)
+
+        x_t = {}
+
+        def x_transpose(pair):
+            x_t[pair] = psum.tile([P, 2, 2, P], F32, name="xt%d" % pair, tag="x_t", bufs=1)
+            for i in range(2):
+                words = x_bf[2 * pair + i][:].bitcast(F32)
+                for u in range(2):
+                    nc.tensor.transpose(x_t[pair][:, i, u, :], words[:, u:256:2], ident[:])
+
+        chunk_of_pair = {}
+        for q, (g, c0, n) in enumerate(CHUNKS):
+            for c in range(c0, c0 + n, 2):
+                chunk_of_pair[(4 * g + c) // 2] = (q, (c - c0) // 2)
+
+        def x_copy(pair):
+            q, half = chunk_of_pair[pair]
+            if half == 0:
+                x_grouped[q] = work.tile([P, 256 * CHUNKS[q][2]], F32, name="xg%d" % q, tag="x_grouped", bufs=2, align_bytes=64)
+            o = x_grouped[q][:, 512 * half : 512 * half + 512].rearrange("p (i r u) -> p i r u", i=2, u=2)
+            i = x_t[pair][:].rearrange("p i u r -> p i r u")
+            if H_ENG[pair] == "V":
+                nc.vector.tensor_copy(out=o, in_=i)
+            else:
+                nc.scalar.copy(out=o, in_=i)
+
+        def x_quantize(q):
+            n = CHUNKS[q][2]
+            x_codes[q] = keep.tile([P, P * n], U32, name="xc%d" % q, align_bytes=64)
+            x_scales[q] = keep.tile([P, P * n], U8, name="xs%d" % q, align_bytes=64)
+            nc.vector.quantize_mx(out=x_codes[q][:].bitcast(E4), scales=x_scales[q][:], in_=x_grouped[q][:].bitcast(BF16))
+
+        steps = [(g, c0, n, hh) for (g, c0, n) in CHUNKS for hh in range(2)]
+        squares, gauss, h_slots, h_grouped, h_codes, h_scales = {}, {}, {}, {}, {}, {}
+
+        def stage1(which, i, t, tag, bufs):
+            g, c0, n, hh = steps[i]
+            acc = psum.tile([P, P * n], F32, name="%s%d_%d" % (tag, i, t), tag="acc", bufs=7)
+            w = slice(P * t, P * t + P)
+            nc.tensor.matmul_mx(out=acc[:], lhsT=w_codes[which, hh][:, w].bitcast(E4), lhsT_scale=w_scales[which, hh][:, w],
+                                rhs=x_codes[i // 2][:].bitcast(E4), rhs_scale=x_scales[i // 2][:], start=True, stop=True)
+            return acc
+
+        def window_square(i, t):
+            g, c0, n, hh = steps[i]
+            if t == 0:
+                squares[i] = work.tile([P, 4, P * n], F32, name="sq%d" % i, tag="squares", bufs=2)
+            acc = stage1("win", i, t, "a", A_BUFS)
+            k = 4 * hh + t
+            nc.scalar.activation(out=squares[i][:, t, :], in_=acc[:], func=ACT.Square,
+                                 scale=win_scale[:, k : k + 1], bias=win_bias[:, k : k + 1])
+
+        def window_exp(i, t0, t1):
+            g, c0, n, hh = steps[i]
+            if t0 == 0:
+                gauss[i] = work.tile([P, 4, P * n], F32, name="ga%d" % i, tag="gauss", bufs=3)
+            nc.scalar.activation(out=gauss[i][:, t0:t1, :], in_=squares[i][:, t0:t1, :], func=ACT.Exp, scale=-0.5)
+
+        def carrier(i, t):
+            g, c0, n, hh = steps[i]
+            if t == 0:
+                h_slots[i] = work.tile([P, 4, P * n], BF16, name="hs%d" % i, tag="h_slots", bufs=3)
+            acc = stage1("car", i, t, "v", V_BUFS)
+            k = 4 * hh + t
+            nc.vector.scalar_tensor_tensor(out=h_slots[i][:, t, :], in0=acc[:], scalar=bias_car[:, k : k + 1],
+                                           in1=gauss[i][:, t, :], op0=ALU.add, op1=ALU.mult)
+
+        def h_interleave(i):
+            n = steps[i][2]
+            h_grouped[i] = work.tile([P, 4 * P * n], BF16, name="hg%d" % i, tag="h_grouped", bufs=2, align_bytes=64)
+            dst = h_grouped[i][:].rearrange("p (n j) -> p n j", j=4)
+            cut = D_G[i] if D_ENG[i] == "G" else P * n
+            interleave(D_ENG[i], dst[:, 0:cut, :], h_slots[i][:, :, 0:cut], False)
+
+        def h_interleave_rest(i):
+            n = steps[i][2]
+            dst = h_grouped[i][:].rearrange("p (n j) -> p n j", j=4)
+            cut = D_G[i] if D_ENG[i] == "G" else P * n
+            if cut < P * n:
+                interleave("V", dst[:, cut:, :], h_slots[i][:, :, cut:], False)
+
+        def h_quantize(i):
+            n = steps[i][2]
+            h_codes[i] = work.tile([P, P * n], U32, name="hc%d" % i, tag="h_codes", bufs=4, align_bytes=64)
+            h_scales[i] = work.tile([P, P * n], U8, name="hsc%d" % i, tag="h_scales", bufs=4, align_bytes=64)
+            nc.vector.quantize_mx(out=h_codes[i][:].bitcast(E5), scales=h_scales[i][:], in_=h_grouped[i][:])
+
+        y_acc, y_sb, slope_sum, normal_sb = {}, {}, {}, {}
+        first_step = {}
+        for i, (g, c0, n, hh) in enumerate(steps):
+            if hh == 0:
+                for c in range(c0, c0 + n):
+                    first_step[4 * g + c] = (i, c - c0)
+
+        def y_matmul(r, h0=0, h1=2):
+            i0, j = first_step[r]
+            if h0 == 0:
+                y_acc[r] = psum.tile([P, PO], F32, name="y%d" % r, tag="acc", bufs=7)
+            cols = slice(P * j, P * j + P)
+            for hh in range(h0, h1):
+                nc.tensor.matmul_mx(out=y_acc[r][:], lhsT=h_codes[i0 + hh][:, cols].bitcast(E5), lhsT_scale=h_scales[i0 + hh][:, cols],
+                                    rhs=w_codes["out", hh][:].bitcast(E4), rhs_scale=w_scales["out", hh][:],
+                                    start=(hh == 0), stop=(hh == 1))
+
+        def y_bias(r, lo=0, hi=PO):
+            pair = r // 2
+            if pair not in y_sb:
+                y_sb[pair] = keep.tile([P, 2, PO], F32, name="ysb%d" % pair)
+            nc.vector.tensor_tensor(out=y_sb[pair][:, r % 2, lo:hi], in0=y_acc[r][:, lo:hi], in1=bias_out[:, lo:hi], op=ALU.add)
+
+        def y_tanh(pair):
+            mat = work.tile([P, 2, S], F32, name="mat%d" % pair, tag="mat", bufs=2)
+            nc.scalar.activation(out=mat[:], in_=y_sb[pair][:, :, 0:S], func=ACT.Tanh)
+            nc.sync.dma_start(out=material_v[:, 2 * pair : 2 * pair + 2, :], in_=mat[:])
+
+        slope_sq = {}
+
+        def slope_square(pair):
+            t = work.tile([P, 2, 2 * D], F32, name="ssq%d" % pair, tag="slope_sq", bufs=2)
+            slope_sq[pair] = t
+            s = y_sb[pair][:, :, S:PO]
+            if SQ_ENG[pair] == "S":
+                nc.scalar.activation(out=t[:], in_=s, func=ACT.Square)
+            else:
+                (nc.vector if SQ_ENG[pair] == "V" else nc.gpsimd).tensor_tensor(out=t[:], in0=s, in1=s, op=ALU.mult)
+
+        sums = keep.tile([P, 16, D], F32, name="sums")
+
+        def slope_add(pair):
+            t = slope_sq[pair]
+            (nc.vector if SUM_ENG[pair] == "V" else nc.gpsimd).tensor_tensor(
+                out=sums[:, 2 * pair : 2 * pair + 2, :], in0=t[:, :, 0:D], in1=t[:, :, D : 2 * D], op=ALU.add)
+
+        normals = keep.tile([P, 16, 3 * D], F32, name="normals")
+
+        def inverse_root(p0, p1):
+            nc.scalar.activation(out=normals[:, 2 * p0 : 2 * p1, 2 * D : 3 * D], in_=sums[:, 2 * p0 : 2 * p1, :],
+                                 func=ACT.Abs_reciprocal_sqrt, bias=1.0)
+
+        def normal_out(pair, store):
+            rows = slice(2 * pair, 2 * pair + 2)
+            eng = nc.vector if MUL_ENG[pair // 2] == "V" else nc.gpsimd
+            eng.tensor_tensor(
+                out=normals[:, rows, 0 : 2 * D].rearrange("p r (a d) -> p r a d", a=2),
+                in0=y_sb[pair][:, :, S:PO].rearrange("p r (a d) -> p r a d", a=2),
+                in1=normals[:, rows, 2 * D : 3 * D].unsqueeze(2).to_broadcast([P, 2, 2, D]), op=ALU.mult)
+            if store:
+                rows = slice(2 * (pair + 1 - store), 2 * pair + 2)
+                nc.sync.dma_start(out=normal_v[:, rows, :], in_=normals[:, rows, :])
+
+        for r in range(4):
+            x_coarse(r)
+        w_interleave(0, 0)
+        w_interleave(0, 1)
+        x_blend(0)
+        x_blend(1)
+        x_transpose(0)
+        x_blend(2)
+        x_blend(3)
+        x_copy(0)
+        x_transpose(1)
+        w_quantize(0)
+        x_coarse(4)
+        x_copy(1)
+        w_interleave(1, 0)
+        w_interleave(1, 1)
+        x_coarse(5)
+        x_quantize(0)
+        w_interleave(2, 0)
+        window_square(0, 0)
+        window_square(0, 1)
+        x_blend(4)
+        x_blend(5)
+        w_quantize(1)
+        x_coarse(6)
+        x_coarse(7)
+        window_square(0, 2)
+        window_square(0, 3)
+        x_transpose(2)
+        w_interleave(2, 1)
+        x_blend(6)
+        x_blend(7)
+        x_copy(2)
+        window_exp(0, 0, 4)
+        w_interleave(3, 0)
+        w_quantize(2)
+        w_interleave(3, 1)
+
+        last = len(steps) - 1
+        y_due = {2: 0, 3: 1, 4: 2, 5: 3, 6: 4, 7: 5, 8: 6}
+        blend_due = {it: pair for pair, it in BLEND_AT.items()}
+        blend_due[-1] = 3
+        for i in range(last):
+            pair_y = y_due.get(i)
+            pair_x = blend_due.get(i)
+            pair_h = blend_due.get(i - 1)
+            pair_t = y_due.get(i - 1)
+            carrier(i, 0)
+            window_square(i + 1, 0)
+            carrier(i, 1)
+            window_square(i + 1, 1)
+            carrier(i, 2)
+            window_square(i + 1, 2)
+            if pair_h is not None:
+                x_transpose(pair_h)
+            if i > 0:
+                h_interleave_rest(i - 1)
+            if i == 0:
+                w_quantize(3)
+            if pair_t is not None and SQ_ENG[pair_t] != "S":
+                slope_square(pair_t)
+            window_square(i + 1, 3)
+            if pair_x is not None:
+                x_coarse(2 * pair_x)
+            if i > 0:
+                h_quantize(i - 1)
+            if pair_x is not None:
+                x_coarse(2 * pair_x + 1)
+            if pair_h is not None:
+                x_copy(pair_h)
+            if pair_t is not None:
+                y_tanh(pair_t)
+            if pair_t is not None and SQ_ENG[pair_t] == "S":
+                slope_square(pair_t)
+            if i < 2:
+                w_interleave(4, i)
+            window_exp(i + 1, 0, 4)
+            if i == 1:
+                w_interleave(5, 0)
+                w_interleave(5, 1)
+            if i == 2:
+                w_quantize(4)
+                w_quantize(5)
+            if pair_x is not None:
+                x_blend(2 * pair_x)
+                x_blend(2 * pair_x + 1)
+            if i % 2 == 0 and i // 2 + 1 < len(CHUNKS):
+                x_quantize(i // 2 + 1)
+            if pair_t is not None:
+                slope_add(pair_t)
+            carrier(i, 3)
+            h_interleave(i)
+            if pair_y is not None:
+                y_matmul(2 * pair_y)
+                y_matmul(2 * pair_y + 1)
+                y_bias(2 * pair_y)
+                y_bias(2 * pair_y + 1)
+
+        y_tanh(6)
+        for t in range(4):
+            carrier(last, t)
+        h_quantize(last - 1)
+        y_matmul(14, 0, 1)
+        y_matmul(15, 0, 1)
+        h_interleave(last)
+        slope_square(6)
+        h_quantize(last)
+        slope_add(6)
+        inverse_root(0, 4)
+        inverse_root(4, 7)
+        y_matmul(14, 1, 2)
+        y_matmul(15, 1, 2)
+        normal_out(0, 0)
+        normal_out(1, 2)
+        y_bias(14, S, PO)
+        y_bias(15, S, PO)
+        normal_out(2, 0)
+        slope_square(7)
+        normal_out(3, 2)
+        slope_add(7)
+        y_bias(14, 0, S)
+        y_bias(15, 0, S)
+        inverse_root(7, 8)
+        for pair in range(4, 8):
+            normal_out(pair, 2 if pair % 2 == 1 else 0)
+        y_tanh(7)

@@ -19,14 +19,19 @@ P = 128
 GROUPS = 4
 CHUNKS = [(0, 0, 4), (1, 0, 4), (2, 0, 4), (3, 0, 2), (3, 2, 2)]
 D_ENG = "GGGGGGGGGV"
-D_G = [320, 320, 512, 512, 512, 352, 256, 256, 256, 0]
+D_G = [192, 192, 384, 384, 384, 256, 192, 192, 256, 0]
+D_REST = "VVVVSSSSVV"
 F_ENG = "VVVVVVVVVVVVVVVV"
 H_ENG = "VVSSSSSS"
 M_ENG = "SSSSSVVVVSSV"
-SQ_ENG = "SSVVVVVV"
+SQ_ENG = "SSVVVVSS"
 SUM_ENG = "VVVVVVVV"
 MUL_ENG = "VVVV"
 BLEND_AT = {4: 0, 5: 1, 6: 3, 7: 4}
+XT_TAG = "acc"
+XT_BUFS = 8
+ACC_BUFS = 8
+M4B = 0
 A_BUFS = 3
 V_BUFS = 2
 Y_BUFS = 2
@@ -61,14 +66,16 @@ def tile_windowed_texture_decoder_f3_kernel(
             fine_sb[g, half] = keep.tile([P, 2, K], BF16, name="fine%d_%d" % (g, half))
             nc.sync.dma_start(out=fine_sb[g, half][:], in_=fine_v[:, g, 2 * half : 2 * half + 2, :])
 
-        def load_w(which, hh, half):
-            t = keep.tile([P, 4, 256], BF16, name="raw_%s%d_%d" % (which, hh, half))
-            w_raw[which, hh, half] = t
+        def load_w(which, hh, halves):
+            width_cols = 256 * len(halves)
+            t = keep.tile([P, 4, width_cols], BF16, name="raw_%s%d_%d" % (which, hh, halves[0]))
+            for half in halves:
+                w_raw[which, hh, half] = t[:, :, 256 * (half - halves[0]) : 256 * (half - halves[0]) + 256]
             if which == "out":
-                src = w_out[512 * hh : 512 * hh + 512, 256 * half : 256 * half + 256]
+                src = w_out[512 * hh : 512 * hh + 512, :]
             else:
-                c0 = 512 * hh + 256 * half
-                src = (w_win if which == "win" else w_car)[:, c0 : c0 + 256]
+                c0 = 512 * hh + 256 * halves[0]
+                src = (w_win if which == "win" else w_car)[:, c0 : c0 + width_cols]
             nc.sync.dma_start(out=t[:], in_=src.rearrange("(p j) n -> p j n", j=4))
 
         def load_channel_vector(vec, name):
@@ -77,20 +84,17 @@ def tile_windowed_texture_decoder_f3_kernel(
             return t[:].rearrange("p h t -> p (h t)")
 
         load_coarse(0)
-        load_w("win", 0, 0)
+        load_w("win", 0, (0,))
         load_fine(0, 0)
-        load_w("win", 0, 1)
+        load_w("win", 0, (1,))
         load_fine(0, 1)
-        load_w("car", 0, 0)
-        load_w("car", 0, 1)
+        load_w("car", 0, (0, 1))
         load_coarse(1)
         load_fine(1, 0)
-        load_w("win", 1, 0)
-        load_w("win", 1, 1)
+        load_w("win", 1, (0, 1))
         load_fine(1, 1)
         for which, hh in (("car", 1), ("out", 0), ("out", 1)):
-            load_w(which, hh, 0)
-            load_w(which, hh, 1)
+            load_w(which, hh, (0, 1))
         bias_out = keep.tile([P, PO], BF16, name="bias_out")
         nc.sync.dma_start(out=bias_out[:], in_=b_out.partition_broadcast(P))
         for g in (2, 3):
@@ -109,8 +113,6 @@ def tile_windowed_texture_decoder_f3_kernel(
         nc.scalar.activation(out=warm_out[:], in_=warm[:], func=ACT.Exp)
         win_scale = keep.tile([P, 8], F32, name="win_scale")
         win_bias = keep.tile([P, 8], F32, name="win_bias")
-        nc.gpsimd.tensor_copy(out=win_scale[:], in_=width_bf)
-        nc.gpsimd.tensor_tensor(out=win_bias[:], in0=width_bf, in1=center_bf, op=ALU.mult)
         lod_f = keep.tile([P, 16], F32, name="lod_f")
         fine_share = keep.tile([P, 16], F32, name="fine_share")
         nc.vector.tensor_copy(out=lod_f[:], in_=lod_sb[:])
@@ -148,7 +150,7 @@ def tile_windowed_texture_decoder_f3_kernel(
                 dst = w_grouped[key][:].rearrange("p (n j) -> p n j", j=4)[:, 256 * half : 256 * half + 256, :]
             else:
                 dst = w_grouped[key][:].rearrange("p (t m j) -> p t m j", t=4, j=4)[:, :, 64 * half : 64 * half + 64, :]
-            interleave(M_ENG[2 * n + half], dst, w_raw[key + (half,)][:], key[0] != "out")
+            interleave(M_ENG[2 * n + half], dst, w_raw[key + (half,)], key[0] != "out")
 
         def w_quantize(n):
             key = w_order[n]
@@ -179,7 +181,7 @@ def tile_windowed_texture_decoder_f3_kernel(
         x_t = {}
 
         def x_transpose(pair):
-            x_t[pair] = psum.tile([P, 2, 2, P], F32, name="xt%d" % pair, tag="x_t", bufs=1)
+            x_t[pair] = psum.tile([P, 2, 2, P], F32, name="xt%d" % pair, tag=XT_TAG, bufs=XT_BUFS)
             for i in range(2):
                 words = x_bf[2 * pair + i][:].bitcast(F32)
                 for u in range(2):
@@ -212,7 +214,7 @@ def tile_windowed_texture_decoder_f3_kernel(
 
         def stage1(which, i, t, tag, bufs):
             g, c0, n, hh = steps[i]
-            acc = psum.tile([P, P * n], F32, name="%s%d_%d" % (tag, i, t), tag="acc", bufs=7)
+            acc = psum.tile([P, P * n], F32, name="%s%d_%d" % (tag, i, t), tag="acc", bufs=ACC_BUFS)
             w = slice(P * t, P * t + P)
             nc.tensor.matmul_mx(out=acc[:], lhsT=w_codes[which, hh][:, w].bitcast(E4), lhsT_scale=w_scales[which, hh][:, w],
                                 rhs=x_codes[i // 2][:].bitcast(E4), rhs_scale=x_scales[i // 2][:], start=True, stop=True)
@@ -233,11 +235,12 @@ def tile_windowed_texture_decoder_f3_kernel(
                 gauss[i] = work.tile([P, 4, P * n], F32, name="ga%d" % i, tag="gauss", bufs=3)
             nc.scalar.activation(out=gauss[i][:, t0:t1, :], in_=squares[i][:, t0:t1, :], func=ACT.Exp, scale=-0.5)
 
-        def carrier(i, t):
+        def carrier(i, t, acc=None):
             g, c0, n, hh = steps[i]
             if t == 0:
                 h_slots[i] = work.tile([P, 4, P * n], BF16, name="hs%d" % i, tag="h_slots", bufs=3)
-            acc = stage1("car", i, t, "v", V_BUFS)
+            if acc is None:
+                acc = stage1("car", i, t, "v", V_BUFS)
             k = 4 * hh + t
             nc.vector.scalar_tensor_tensor(out=h_slots[i][:, t, :], in0=acc[:], scalar=bias_car[:, k : k + 1],
                                            in1=gauss[i][:, t, :], op0=ALU.add, op1=ALU.mult)
@@ -254,7 +257,7 @@ def tile_windowed_texture_decoder_f3_kernel(
             dst = h_grouped[i][:].rearrange("p (n j) -> p n j", j=4)
             cut = D_G[i] if D_ENG[i] == "G" else P * n
             if cut < P * n:
-                interleave("V", dst[:, cut:, :], h_slots[i][:, :, cut:], False)
+                interleave(D_REST[i], dst[:, cut:, :], h_slots[i][:, :, cut:], False)
 
         def h_quantize(i):
             n = steps[i][2]
@@ -272,7 +275,7 @@ def tile_windowed_texture_decoder_f3_kernel(
         def y_matmul(r, h0=0, h1=2):
             i0, j = first_step[r]
             if h0 == 0:
-                y_acc[r] = psum.tile([P, PO], F32, name="y%d" % r, tag="acc", bufs=7)
+                y_acc[r] = psum.tile([P, PO], F32, name="y%d" % r, tag="acc", bufs=ACC_BUFS)
             cols = slice(P * j, P * j + P)
             for hh in range(h0, h1):
                 nc.tensor.matmul_mx(out=y_acc[r][:], lhsT=h_codes[i0 + hh][:, cols].bitcast(E5), lhsT_scale=h_scales[i0 + hh][:, cols],
@@ -285,10 +288,10 @@ def tile_windowed_texture_decoder_f3_kernel(
                 y_sb[pair] = keep.tile([P, 2, PO], F32, name="ysb%d" % pair)
             nc.vector.tensor_tensor(out=y_sb[pair][:, r % 2, lo:hi], in0=y_acc[r][:, lo:hi], in1=bias_out[:, lo:hi], op=ALU.add)
 
-        def y_tanh(pair):
-            mat = work.tile([P, 2, S], F32, name="mat%d" % pair, tag="mat", bufs=2)
-            nc.scalar.activation(out=mat[:], in_=y_sb[pair][:, :, 0:S], func=ACT.Tanh)
-            nc.sync.dma_start(out=material_v[:, 2 * pair : 2 * pair + 2, :], in_=mat[:])
+        def y_tanh(pair, r0=0, r1=2):
+            mat = work.tile([P, r1 - r0, S], F32, name="mat%d_%d" % (pair, r0), tag="mat", bufs=3)
+            nc.scalar.activation(out=mat[:], in_=y_sb[pair][:, r0:r1, 0:S], func=ACT.Tanh)
+            nc.sync.dma_start(out=material_v[:, 2 * pair + r0 : 2 * pair + r1, :], in_=mat[:])
 
         slope_sq = {}
 
@@ -337,6 +340,8 @@ def tile_windowed_texture_decoder_f3_kernel(
         x_copy(0)
         x_transpose(1)
         w_quantize(0)
+        nc.vector.tensor_copy(out=win_scale[:], in_=width_bf)
+        nc.vector.tensor_tensor(out=win_bias[:], in0=width_bf, in1=center_bf, op=ALU.mult)
         x_coarse(4)
         x_copy(1)
         w_interleave(1, 0)
@@ -348,9 +353,9 @@ def tile_windowed_texture_decoder_f3_kernel(
         window_square(0, 1)
         x_blend(4)
         x_blend(5)
-        w_quantize(1)
         x_coarse(6)
         x_coarse(7)
+        w_quantize(1)
         window_square(0, 2)
         window_square(0, 3)
         x_transpose(2)
@@ -359,67 +364,80 @@ def tile_windowed_texture_decoder_f3_kernel(
         x_blend(7)
         x_copy(2)
         window_exp(0, 0, 4)
-        w_interleave(3, 0)
         w_quantize(2)
+        x_coarse(8)
+        x_coarse(9)
+        w_interleave(3, 0)
         w_interleave(3, 1)
+        w_interleave(4, 0)
+        window_square(1, 0)
+        window_square(1, 1)
 
         last = len(steps) - 1
         y_due = {2: 0, 3: 1, 4: 2, 5: 3, 6: 4, 7: 5, 8: 6}
         blend_due = {it: pair for pair, it in BLEND_AT.items()}
         blend_due[-1] = 3
         for i in range(last):
+            pair_h = blend_due.get(i - 1)
             pair_y = y_due.get(i)
             pair_x = blend_due.get(i)
-            pair_h = blend_due.get(i - 1)
+            pair_f = blend_due.get(i + 1)
             pair_t = y_due.get(i - 1)
             carrier(i, 0)
-            window_square(i + 1, 0)
             carrier(i, 1)
-            window_square(i + 1, 1)
-            carrier(i, 2)
-            window_square(i + 1, 2)
             if pair_h is not None:
                 x_transpose(pair_h)
-            if i > 0:
+                x_copy(pair_h)
+            carrier(i, 2)
+            window_square(i + 1, 2)
+            window_square(i + 1, 3)
+            acc_last = stage1("car", i, 3, "v", V_BUFS)
+            if i > 0 and D_REST[i - 1] == "V":
                 h_interleave_rest(i - 1)
-            if i == 0:
-                w_quantize(3)
             if pair_t is not None and SQ_ENG[pair_t] != "S":
                 slope_square(pair_t)
-            window_square(i + 1, 3)
-            if pair_x is not None:
-                x_coarse(2 * pair_x)
+            if pair_f is not None:
+                x_coarse(2 * pair_f)
+            if i == 0:
+                w_quantize(3)
+            if i == 2:
+                w_quantize(4)
+                w_quantize(5)
+            if pair_y is not None:
+                y_matmul(2 * pair_y, 0, 1)
+                y_matmul(2 * pair_y + 1, 0, 1)
             if i > 0:
                 h_quantize(i - 1)
-            if pair_x is not None:
-                x_coarse(2 * pair_x + 1)
-            if pair_h is not None:
-                x_copy(pair_h)
+            if i % 2 == 0 and i // 2 + 1 < len(CHUNKS):
+                x_quantize(i // 2 + 1)
+            if pair_y is not None:
+                y_matmul(2 * pair_y, 1, 2)
+                y_matmul(2 * pair_y + 1, 1, 2)
             if pair_t is not None:
                 y_tanh(pair_t)
             if pair_t is not None and SQ_ENG[pair_t] == "S":
                 slope_square(pair_t)
-            if i < 2:
-                w_interleave(4, i)
+            if i == M4B:
+                w_interleave(4, 1)
             window_exp(i + 1, 0, 4)
-            if i == 1:
-                w_interleave(5, 0)
-                w_interleave(5, 1)
-            if i == 2:
-                w_quantize(4)
-                w_quantize(5)
             if pair_x is not None:
                 x_blend(2 * pair_x)
                 x_blend(2 * pair_x + 1)
-            if i % 2 == 0 and i // 2 + 1 < len(CHUNKS):
-                x_quantize(i // 2 + 1)
+            if i == 1:
+                w_interleave(5, 0)
+                w_interleave(5, 1)
+            if pair_f is not None:
+                x_coarse(2 * pair_f + 1)
             if pair_t is not None:
                 slope_add(pair_t)
-            carrier(i, 3)
+            carrier(i, 3, acc_last)
             h_interleave(i)
+            if i + 2 <= last:
+                window_square(i + 2, 0)
+                window_square(i + 2, 1)
+            if D_REST[i] == "S":
+                h_interleave_rest(i)
             if pair_y is not None:
-                y_matmul(2 * pair_y)
-                y_matmul(2 * pair_y + 1)
                 y_bias(2 * pair_y)
                 y_bias(2 * pair_y + 1)
 
@@ -430,24 +448,26 @@ def tile_windowed_texture_decoder_f3_kernel(
         y_matmul(14, 0, 1)
         y_matmul(15, 0, 1)
         h_interleave(last)
+        inverse_root(0, 2)
+        inverse_root(2, 4)
         slope_square(6)
         h_quantize(last)
-        slope_add(6)
-        inverse_root(0, 4)
-        inverse_root(4, 7)
         y_matmul(14, 1, 2)
         y_matmul(15, 1, 2)
         normal_out(0, 0)
         normal_out(1, 2)
+        slope_add(6)
+        inverse_root(4, 7)
         y_bias(14, S, PO)
         y_bias(15, S, PO)
-        normal_out(2, 0)
         slope_square(7)
+        normal_out(2, 0)
         normal_out(3, 2)
         slope_add(7)
+        inverse_root(7, 8)
         y_bias(14, 0, S)
         y_bias(15, 0, S)
-        inverse_root(7, 8)
         for pair in range(4, 8):
             normal_out(pair, 2 if pair % 2 == 1 else 0)
-        y_tanh(7)
+        y_tanh(7, 0, 1)
+        y_tanh(7, 1, 2)

@@ -3,38 +3,28 @@ from contextlib import ExitStack
 import concourse.mybir as mybir
 from concourse.masks import make_identity
 
-M, K, N, PO, S, D = 2048, 512, 1024, 512, 384, 64
-FLOPS = 2 * M * K * N * 2 + 2 * M * N * PO
+M, K, N, OUT, PLANES, SUB = 2048, 512, 1024, 512, 384, 64
+FLOPS = 2 * M * K * N * 2 + 2 * M * N * OUT
 
 F32 = mybir.dt.float32
 BF16 = mybir.dt.bfloat16
 U32 = mybir.dt.uint32
 U8 = mybir.dt.uint8
-E4 = mybir.dt.float8_e4m3fn_x4
-E5 = mybir.dt.float8_e5m2_x4
+E4M3 = mybir.dt.float8_e4m3fn_x4
+E5M2 = mybir.dt.float8_e5m2_x4
 ALU = mybir.AluOpType
 ACT = mybir.ActivationFunctionType
 
 P = 128
-GROUPS = 4
-CHUNKS = [(0, 0, 4), (1, 0, 4), (2, 0, 4), (3, 0, 2), (3, 2, 2)]
-D_ENG = "GGGGGGGGGV"
-D_G = [192, 192, 384, 384, 384, 256, 192, 192, 256, 0]
-D_REST = "VVVVSSSSVV"
-F_ENG = "VVVVVVVVVVVVVVVV"
-H_ENG = "VVSSSSSS"
-M_ENG = "SSSSSVVVVSSV"
-SQ_ENG = "SSVVVVSS"
-SUM_ENG = "VVVVVVVV"
-MUL_ENG = "VVVV"
-BLEND_AT = {4: 0, 5: 1, 6: 3, 7: 4}
-XT_TAG = "acc"
-XT_BUFS = 8
-ACC_BUFS = 8
-M4B = 0
-A_BUFS = 3
-V_BUFS = 2
-Y_BUFS = 2
+SLOTS = 4
+PASS = P * SLOTS
+ROWS = M // P
+PAIRS = ROWS // 2
+PART = 256
+CHUNKS = [(0, 4), (4, 4), (8, 4), (12, 2), (14, 2)]
+GPSIMD_RATE = 3 / 16
+GPSIMD_LEAD = 512
+SCALAR_REST_FROM = 4
 
 
 def tile_windowed_texture_decoder_f3_kernel(
@@ -44,430 +34,402 @@ def tile_windowed_texture_decoder_f3_kernel(
     with ExitStack() as ctx:
         keep = ctx.enter_context(tc.tile_pool(name="keep", bufs=1))
         work = ctx.enter_context(tc.tile_pool(name="work", bufs=2))
-        psum = ctx.enter_context(tc.psum_pool(name="psum", bufs=1))
+        psum = ctx.enter_context(tc.psum_pool(name="psum", bufs=8))
         ctx.enter_context(tc.manual_schedule())
 
-        fine_v = fine.rearrange("(p g c) k -> p g c k", g=GROUPS, c=4)
-        coarse_v = coarse.rearrange("(p g) k -> p g k", g=GROUPS)
-        material_v = material.rearrange("(p r) s -> p r s", r=16)
-        normal_v = normal.rearrange("(p r) s -> p r s", r=16)
+        fine_rows = fine.rearrange("(p r) k -> p r k", r=ROWS)
+        coarse_rows = coarse.rearrange("(p g) k -> p g k", g=ROWS // 4)
+        material_rows = material.rearrange("(p r) s -> p r s", r=ROWS)
+        normal_rows = normal.rearrange("(p r) s -> p r s", r=ROWS)
 
-        lod_sb = keep.tile([P, 16], BF16, name="lod_sb")
-        nc.sync.dma_start(out=lod_sb[:], in_=lod.rearrange("(p r) -> p r", r=16))
-        coarse_sb = {}
-        fine_sb = {}
-        w_raw = {}
+        zero = keep.tile([P, 1], F32, name="zero")
+        one = keep.tile([P, 1], F32, name="one")
+        nc.vector.memset(zero[:], 0.0)
+        nc.scalar.activation(out=one[:], in_=zero[:], func=ACT.Exp)
 
-        def load_coarse(g):
-            coarse_sb[g] = keep.tile([P, K], BF16, name="coarse%d" % g)
-            nc.sync.dma_start(out=coarse_sb[g][:], in_=coarse_v[:, g, :])
+        coarse_sb, fine_sb, w_raw = {}, {}, {}
 
-        def load_fine(g, half):
-            fine_sb[g, half] = keep.tile([P, 2, K], BF16, name="fine%d_%d" % (g, half))
-            nc.sync.dma_start(out=fine_sb[g, half][:], in_=fine_v[:, g, 2 * half : 2 * half + 2, :])
+        def load_coarse(group):
+            coarse_sb[group] = keep.tile([P, K], BF16, name="coarse%d" % group)
+            nc.sync.dma_start(out=coarse_sb[group][:], in_=coarse_rows[:, group, :])
 
-        def load_w(which, hh, halves):
-            width_cols = 256 * len(halves)
-            t = keep.tile([P, 4, width_cols], BF16, name="raw_%s%d_%d" % (which, hh, halves[0]))
-            for half in halves:
-                w_raw[which, hh, half] = t[:, :, 256 * (half - halves[0]) : 256 * (half - halves[0]) + 256]
+        def load_fine(pair):
+            fine_sb[pair] = keep.tile([P, 2, K], BF16, name="fine%d" % pair)
+            nc.sync.dma_start(out=fine_sb[pair][:], in_=fine_rows[:, 2 * pair : 2 * pair + 2, :])
+
+        def load_weight(which, half, parts=(0, 1)):
+            cols = PART * len(parts)
+            raw = keep.tile([P, SLOTS, cols], BF16, name="raw_%s%d_%d" % (which, half, parts[0]))
+            for n, part in enumerate(parts):
+                w_raw[which, half, part] = raw[:, :, PART * n : PART * n + PART]
             if which == "out":
-                src = w_out[512 * hh : 512 * hh + 512, :]
+                src = w_out[PASS * half : PASS * half + PASS, :]
             else:
-                c0 = 512 * hh + 256 * halves[0]
-                src = (w_win if which == "win" else w_car)[:, c0 : c0 + width_cols]
-            nc.sync.dma_start(out=t[:], in_=src.rearrange("(p j) n -> p j n", j=4))
+                first = PASS * half + PART * parts[0]
+                src = (w_win if which == "win" else w_car)[:, first : first + cols]
+            nc.sync.dma_start(out=raw[:], in_=src.rearrange("(p t) n -> p t n", t=SLOTS))
 
-        def load_channel_vector(vec, name):
-            t = keep.tile([P, 2, 4], BF16, name=name)
-            nc.gpsimd.dma_start(out=t[:], in_=vec.rearrange("(h p t) -> p h t", h=2, t=4))
-            return t[:].rearrange("p h t -> p (h t)")
+        def load_hidden_vector(vec, name):
+            tile = keep.tile([P, 2, SLOTS], BF16, name=name)
+            nc.gpsimd.dma_start(out=tile[:], in_=vec.rearrange("(h p t) -> p h t", h=2, t=SLOTS))
+            return tile[:].rearrange("p h t -> p (h t)")
 
+        lod_bf = keep.tile([P, ROWS], BF16, name="lod_bf")
+        nc.sync.dma_start(out=lod_bf[:], in_=lod.rearrange("(p r) -> p r", r=ROWS))
         load_coarse(0)
-        load_w("win", 0, (0,))
-        load_fine(0, 0)
-        load_w("win", 0, (1,))
-        load_fine(0, 1)
-        load_w("car", 0, (0, 1))
+        load_weight("win", 0, (0,))
+        load_fine(0)
+        load_weight("win", 0, (1,))
+        load_fine(1)
+        load_weight("car", 0)
         load_coarse(1)
-        load_fine(1, 0)
-        load_w("win", 1, (0, 1))
-        load_fine(1, 1)
-        for which, hh in (("car", 1), ("out", 0), ("out", 1)):
-            load_w(which, hh, (0, 1))
-        bias_out = keep.tile([P, PO], BF16, name="bias_out")
+        load_fine(2)
+        load_weight("win", 1)
+        load_fine(3)
+        load_weight("car", 1)
+        load_weight("out", 0)
+        load_weight("out", 1)
+        bias_out = keep.tile([P, OUT], BF16, name="bias_out")
         nc.sync.dma_start(out=bias_out[:], in_=b_out.partition_broadcast(P))
-        for g in (2, 3):
-            load_coarse(g)
-            load_fine(g, 0)
-            load_fine(g, 1)
+        for group in (2, 3):
+            load_coarse(group)
+            load_fine(2 * group)
+            load_fine(2 * group + 1)
+        width_bf = load_hidden_vector(width, "width_bf")
+        center_bf = load_hidden_vector(center, "center_bf")
+        bias_car = load_hidden_vector(b_car, "bias_car")
 
-        width_bf = load_channel_vector(width, "width_bf")
-        center_bf = load_channel_vector(center, "center_bf")
-        bias_car = load_channel_vector(b_car, "bias_car")
-        ident = keep.tile([P, P], F32, name="ident")
-        make_identity(nc, ident[:])
-        warm = keep.tile([P, 1], F32, name="warm")
-        warm_out = keep.tile([P, 1], F32, name="warm_out")
-        nc.vector.memset(warm[:], 0.0)
-        nc.scalar.activation(out=warm_out[:], in_=warm[:], func=ACT.Exp)
-        win_scale = keep.tile([P, 8], F32, name="win_scale")
-        win_bias = keep.tile([P, 8], F32, name="win_bias")
-        lod_f = keep.tile([P, 16], F32, name="lod_f")
-        fine_share = keep.tile([P, 16], F32, name="fine_share")
-        nc.vector.tensor_copy(out=lod_f[:], in_=lod_sb[:])
-        nc.vector.tensor_scalar(out=fine_share[:], in0=lod_sb[:], scalar1=-1.0, scalar2=1.0, op0=ALU.mult, op1=ALU.add)
+        identity = keep.tile([P, P], F32, name="identity")
+        make_identity(nc, identity[:])
+        coarse_share = keep.tile([P, ROWS], F32, name="coarse_share")
+        fine_share = keep.tile([P, ROWS], F32, name="fine_share")
+        nc.vector.tensor_copy(out=coarse_share[:], in_=lod_bf[:])
+        nc.vector.tensor_scalar(
+            out=fine_share[:], in0=lod_bf[:], scalar1=-1.0, scalar2=1.0, op0=ALU.mult, op1=ALU.add
+        )
 
-        def interleave(eng, dst, src, permute):
-            if eng == "G":
-                if permute:
-                    o = dst
-                    i = src.rearrange("p j (m t) -> p t m j", t=4)
-                else:
-                    o = dst
-                    i = src.rearrange("p j n -> p n j")
-                nc.gpsimd.tensor_scalar(out=o, in0=i, scalar1=1.0, scalar2=0.0, op0=ALU.mult, op1=ALU.add)
-                return
-            if permute:
-                o = dst.rearrange("p t (m i) j -> p m t i j", i=2)
-                i = src.rearrange("p j (m i t) -> p m t i j", i=2, t=4)
+        def move(engine, out, in_):
+            if engine == "vector":
+                nc.vector.tensor_copy(out=out, in_=in_)
+            elif engine == "scalar":
+                nc.scalar.copy(out=out, in_=in_)
             else:
-                o = dst.rearrange("p (c i) j -> p c j i", i=4)
-                i = src.rearrange("p j (c i) -> p c j i", i=4)
-            if eng == "V":
-                nc.vector.tensor_copy(out=o, in_=i)
+                nc.gpsimd.tensor_scalar(out=out, in0=in_, scalar1=1.0, scalar2=0.0, op0=ALU.mult, op1=ALU.add)
+
+        def quantize(grouped, dtype, pool, name, tag="", bufs=None):
+            cols = grouped.shape[1] // SLOTS
+            codes = pool.tile([P, cols], U32, name=name + "_codes", tag=tag and tag + "_codes", bufs=bufs, align_bytes=64)
+            scales = pool.tile([P, cols], U8, name=name + "_scales", tag=tag and tag + "_scales", bufs=bufs, align_bytes=64)
+            nc.vector.quantize_mx(out=codes[:].bitcast(dtype), scales=scales[:], in_=grouped)
+            return codes, scales
+
+        w_grouped, w_mx = {}, {}
+
+        def weight_interleave(which, half, part, engine):
+            if part == 0:
+                w_grouped[which, half] = work.tile(
+                    [P, SLOTS * PASS], BF16, name="grouped_%s%d" % (which, half), tag="w_grouped", bufs=3, align_bytes=64
+                )
+            grouped = w_grouped[which, half][:]
+            raw = w_raw[which, half, part]
+            if which == "out":
+                dst = grouped.rearrange("p (n t) -> p n t", t=SLOTS)[:, PART * part : PART * part + PART, :]
+                move(engine, dst, raw.rearrange("p t n -> p n t"))
             else:
-                nc.scalar.copy(out=o, in_=i)
+                m0 = PART // SLOTS * part
+                dst = grouped.rearrange("p (s m t) -> p s m t", s=SLOTS, t=SLOTS)[:, :, m0 : m0 + PART // SLOTS, :]
+                move(
+                    engine,
+                    dst.rearrange("p s (m i) t -> p m s i t", i=2),
+                    raw.rearrange("p t (m i s) -> p m s i t", i=2, s=SLOTS),
+                )
 
-        w_order = [("win", 0), ("car", 0), ("win", 1), ("car", 1), ("out", 0), ("out", 1)]
-        w_grouped, w_codes, w_scales = {}, {}, {}
+        def weight_quantize(which, half):
+            w_mx[which, half] = quantize(w_grouped[which, half][:], E4M3, keep, "w_%s%d" % (which, half))
 
-        def w_interleave(n, half):
-            key = w_order[n]
-            if half == 0:
-                w_grouped[key] = work.tile([P, 2048], BF16, name="wg%d" % n, tag="w_grouped", bufs=3, align_bytes=64)
-            if key[0] == "out":
-                dst = w_grouped[key][:].rearrange("p (n j) -> p n j", j=4)[:, 256 * half : 256 * half + 256, :]
-            else:
-                dst = w_grouped[key][:].rearrange("p (t m j) -> p t m j", t=4, j=4)[:, :, 64 * half : 64 * half + 64, :]
-            interleave(M_ENG[2 * n + half], dst, w_raw[key + (half,)], key[0] != "out")
+        coarse_part, x_bf, x_turned, x_grouped, x_mx = {}, {}, {}, {}, {}
+        chunk_of_row = {r: q for q, (first, rows) in enumerate(CHUNKS) for r in range(first, first + rows)}
 
-        def w_quantize(n):
-            key = w_order[n]
-            w_codes[key] = keep.tile([P, 512], U32, name="wc%d" % n, align_bytes=64)
-            w_scales[key] = keep.tile([P, 512], U8, name="ws%d" % n, align_bytes=64)
-            nc.vector.quantize_mx(out=w_codes[key][:].bitcast(E4), scales=w_scales[key][:], in_=w_grouped[key][:])
+        def x_coarse(row):
+            coarse_part[row] = work.tile([P, K], F32, name="coarse_part%d" % row, tag="coarse_part", bufs=4)
+            nc.vector.tensor_scalar(
+                out=coarse_part[row][:], in0=coarse_sb[row // 4][:], scalar1=coarse_share[:, row : row + 1],
+                scalar2=None, op0=ALU.mult,
+            )
 
-        coarse_part, x_bf, x_grouped, x_codes, x_scales = {}, {}, {}, {}, {}
-
-        def x_coarse(r):
-            g = r // 4
-            t = work.tile([P, K], F32, name="cp%d" % r, tag="coarse_part", bufs=4)
-            coarse_part[r] = t
-            if F_ENG[r] == "V":
-                nc.vector.tensor_scalar(out=t[:], in0=coarse_sb[g][:], scalar1=lod_f[:, r : r + 1], scalar2=None, op0=ALU.mult)
-            elif F_ENG[r] == "G":
-                nc.gpsimd.tensor_scalar(out=t[:], in0=coarse_sb[g][:], scalar1=lod_f[:, r : r + 1], scalar2=0.0, op0=ALU.mult, op1=ALU.add)
-            else:
-                nc.scalar.activation(out=t[:], in_=coarse_sb[g][:], func=ACT.Copy, scale=lod_f[:, r : r + 1])
-
-        def x_blend(r):
-            g, c = divmod(r, 4)
-            x_bf[r] = work.tile([P, K], BF16, name="xb%d" % r, tag="x_bf", bufs=4)
+        def x_blend(row):
+            x_bf[row] = work.tile([P, K], BF16, name="x_bf%d" % row, tag="x_bf", bufs=4)
             nc.vector.scalar_tensor_tensor(
-                out=x_bf[r][:], in0=fine_sb[g, c // 2][:, c % 2, :], scalar=fine_share[:, r : r + 1],
-                in1=coarse_part[r][:], op0=ALU.mult, op1=ALU.add)
-
-        x_t = {}
+                out=x_bf[row][:], in0=fine_sb[row // 2][:, row % 2, :], scalar=fine_share[:, row : row + 1],
+                in1=coarse_part[row][:], op0=ALU.mult, op1=ALU.add,
+            )
 
         def x_transpose(pair):
-            x_t[pair] = psum.tile([P, 2, 2, P], F32, name="xt%d" % pair, tag=XT_TAG, bufs=XT_BUFS)
-            for i in range(2):
-                words = x_bf[2 * pair + i][:].bitcast(F32)
+            x_turned[pair] = psum.tile([P, 2, 2, P], F32, name="x_turned%d" % pair, tag="bank")
+            for j in range(2):
+                words = x_bf[2 * pair + j][:].bitcast(F32)
                 for u in range(2):
-                    nc.tensor.transpose(x_t[pair][:, i, u, :], words[:, u:256:2], ident[:])
+                    nc.tensor.transpose(x_turned[pair][:, j, u, :], words[:, u : K // 2 : 2], identity[:])
 
-        chunk_of_pair = {}
-        for q, (g, c0, n) in enumerate(CHUNKS):
-            for c in range(c0, c0 + n, 2):
-                chunk_of_pair[(4 * g + c) // 2] = (q, (c - c0) // 2)
-
-        def x_copy(pair):
-            q, half = chunk_of_pair[pair]
-            if half == 0:
-                x_grouped[q] = work.tile([P, 256 * CHUNKS[q][2]], F32, name="xg%d" % q, tag="x_grouped", bufs=2, align_bytes=64)
-            o = x_grouped[q][:, 512 * half : 512 * half + 512].rearrange("p (i r u) -> p i r u", i=2, u=2)
-            i = x_t[pair][:].rearrange("p i u r -> p i r u")
-            if H_ENG[pair] == "V":
-                nc.vector.tensor_copy(out=o, in_=i)
-            else:
-                nc.scalar.copy(out=o, in_=i)
+        def x_copy(pair, engine):
+            q = chunk_of_row[2 * pair]
+            first, rows = CHUNKS[q]
+            if 2 * pair == first:
+                x_grouped[q] = work.tile([P, 2 * P * rows], F32, name="x_grouped%d" % q, tag="x_grouped", align_bytes=64)
+            w0 = 2 * P * (2 * pair - first)
+            dst = x_grouped[q][:, w0 : w0 + 4 * P].rearrange("p (j c u) -> p j c u", j=2, u=2)
+            move(engine, dst, x_turned[pair][:].rearrange("p j u c -> p j c u"))
 
         def x_quantize(q):
-            n = CHUNKS[q][2]
-            x_codes[q] = keep.tile([P, P * n], U32, name="xc%d" % q, align_bytes=64)
-            x_scales[q] = keep.tile([P, P * n], U8, name="xs%d" % q, align_bytes=64)
-            nc.vector.quantize_mx(out=x_codes[q][:].bitcast(E4), scales=x_scales[q][:], in_=x_grouped[q][:].bitcast(BF16))
+            x_mx[q] = quantize(x_grouped[q][:].bitcast(BF16), E4M3, keep, "x%d" % q)
 
-        steps = [(g, c0, n, hh) for (g, c0, n) in CHUNKS for hh in range(2)]
-        squares, gauss, h_slots, h_grouped, h_codes, h_scales = {}, {}, {}, {}, {}, {}
+        last = 2 * len(CHUNKS) - 1
+        texels = [P * CHUNKS[i // 2][1] for i in range(last + 1)]
+        window_scale = keep.tile([P, 2 * SLOTS], F32, name="window_scale")
+        window_bias = keep.tile([P, 2 * SLOTS], F32, name="window_bias")
+        squares, gauss, h_slots, h_grouped, h_mx = {}, {}, {}, {}, {}
 
-        def stage1(which, i, t, tag, bufs):
-            g, c0, n, hh = steps[i]
-            acc = psum.tile([P, P * n], F32, name="%s%d_%d" % (tag, i, t), tag="acc", bufs=ACC_BUFS)
-            w = slice(P * t, P * t + P)
-            nc.tensor.matmul_mx(out=acc[:], lhsT=w_codes[which, hh][:, w].bitcast(E4), lhsT_scale=w_scales[which, hh][:, w],
-                                rhs=x_codes[i // 2][:].bitcast(E4), rhs_scale=x_scales[i // 2][:], start=True, stop=True)
+        def first_stage(which, i, t):
+            acc = psum.tile([P, texels[i]], F32, name="%s%d_%d" % (which, i, t), tag="bank")
+            w_codes, w_scales = w_mx[which, i % 2]
+            x_codes, x_scales = x_mx[i // 2]
+            cols = slice(P * t, P * t + P)
+            nc.tensor.matmul_mx(
+                out=acc[:], lhsT=w_codes[:, cols].bitcast(E4M3), lhsT_scale=w_scales[:, cols],
+                rhs=x_codes[:].bitcast(E4M3), rhs_scale=x_scales[:], start=True, stop=True,
+            )
             return acc
 
         def window_square(i, t):
-            g, c0, n, hh = steps[i]
             if t == 0:
-                squares[i] = work.tile([P, 4, P * n], F32, name="sq%d" % i, tag="squares", bufs=2)
-            acc = stage1("win", i, t, "a", A_BUFS)
-            k = 4 * hh + t
-            nc.scalar.activation(out=squares[i][:, t, :], in_=acc[:], func=ACT.Square,
-                                 scale=win_scale[:, k : k + 1], bias=win_bias[:, k : k + 1])
+                squares[i] = work.tile([P, SLOTS, texels[i]], F32, name="squares%d" % i, tag="squares")
+            acc = first_stage("win", i, t)
+            col = slice(SLOTS * (i % 2) + t, SLOTS * (i % 2) + t + 1)
+            nc.scalar.activation(
+                out=squares[i][:, t, :], in_=acc[:], func=ACT.Square, scale=window_scale[:, col], bias=window_bias[:, col]
+            )
 
-        def window_exp(i, t0, t1):
-            g, c0, n, hh = steps[i]
-            if t0 == 0:
-                gauss[i] = work.tile([P, 4, P * n], F32, name="ga%d" % i, tag="gauss", bufs=3)
-            nc.scalar.activation(out=gauss[i][:, t0:t1, :], in_=squares[i][:, t0:t1, :], func=ACT.Exp, scale=-0.5)
+        def window_exp(i):
+            gauss[i] = work.tile([P, SLOTS, texels[i]], F32, name="gauss%d" % i, tag="gauss", bufs=3)
+            nc.scalar.activation(out=gauss[i][:], in_=squares[i][:], func=ACT.Exp, scale=-0.5)
 
-        def carrier(i, t, acc=None):
-            g, c0, n, hh = steps[i]
+        def h_product(i, t, acc):
             if t == 0:
-                h_slots[i] = work.tile([P, 4, P * n], BF16, name="hs%d" % i, tag="h_slots", bufs=3)
-            if acc is None:
-                acc = stage1("car", i, t, "v", V_BUFS)
-            k = 4 * hh + t
-            nc.vector.scalar_tensor_tensor(out=h_slots[i][:, t, :], in0=acc[:], scalar=bias_car[:, k : k + 1],
-                                           in1=gauss[i][:, t, :], op0=ALU.add, op1=ALU.mult)
+                h_slots[i] = work.tile([P, SLOTS, texels[i]], BF16, name="h_slots%d" % i, tag="h_slots", bufs=3)
+            col = slice(SLOTS * (i % 2) + t, SLOTS * (i % 2) + t + 1)
+            nc.vector.scalar_tensor_tensor(
+                out=h_slots[i][:, t, :], in0=acc[:], scalar=bias_car[:, col], in1=gauss[i][:, t, :],
+                op0=ALU.add, op1=ALU.mult,
+            )
 
-        def h_interleave(i):
-            n = steps[i][2]
-            h_grouped[i] = work.tile([P, 4 * P * n], BF16, name="hg%d" % i, tag="h_grouped", bufs=2, align_bytes=64)
-            dst = h_grouped[i][:].rearrange("p (n j) -> p n j", j=4)
-            cut = D_G[i] if D_ENG[i] == "G" else P * n
-            interleave(D_ENG[i], dst[:, 0:cut, :], h_slots[i][:, :, 0:cut], False)
+        def carrier(i, t):
+            h_product(i, t, first_stage("car", i, t))
 
-        def h_interleave_rest(i):
-            n = steps[i][2]
-            dst = h_grouped[i][:].rearrange("p (n j) -> p n j", j=4)
-            cut = D_G[i] if D_ENG[i] == "G" else P * n
-            if cut < P * n:
-                interleave(D_REST[i], dst[:, cut:, :], h_slots[i][:, :, cut:], False)
+        def h_interleave(i, engine, c0, c1):
+            if c0 == 0:
+                h_grouped[i] = work.tile([P, texels[i], SLOTS], BF16, name="h_grouped%d" % i, tag="h_grouped", align_bytes=64)
+            move(engine, h_grouped[i][:, c0:c1, :], h_slots[i][:, :, c0:c1].rearrange("p t c -> p c t"))
 
         def h_quantize(i):
-            n = steps[i][2]
-            h_codes[i] = work.tile([P, P * n], U32, name="hc%d" % i, tag="h_codes", bufs=4, align_bytes=64)
-            h_scales[i] = work.tile([P, P * n], U8, name="hsc%d" % i, tag="h_scales", bufs=4, align_bytes=64)
-            nc.vector.quantize_mx(out=h_codes[i][:].bitcast(E5), scales=h_scales[i][:], in_=h_grouped[i][:])
+            h_mx[i] = quantize(h_grouped[i][:].rearrange("p c t -> p (c t)"), E5M2, work, "h%d" % i, tag="h", bufs=4)
 
-        y_acc, y_sb, slope_sum, normal_sb = {}, {}, {}, {}
-        first_step = {}
-        for i, (g, c0, n, hh) in enumerate(steps):
-            if hh == 0:
-                for c in range(c0, c0 + n):
-                    first_step[4 * g + c] = (i, c - c0)
+        y_acc, y_sb, slope_squares = {}, {}, {}
+        slope_sums = keep.tile([P, ROWS, SUB], F32, name="slope_sums")
+        normals = keep.tile([P, ROWS, 3 * SUB], F32, name="normals")
 
-        def y_matmul(r, h0=0, h1=2):
-            i0, j = first_step[r]
-            if h0 == 0:
-                y_acc[r] = psum.tile([P, PO], F32, name="y%d" % r, tag="acc", bufs=ACC_BUFS)
-            cols = slice(P * j, P * j + P)
-            for hh in range(h0, h1):
-                nc.tensor.matmul_mx(out=y_acc[r][:], lhsT=h_codes[i0 + hh][:, cols].bitcast(E5), lhsT_scale=h_scales[i0 + hh][:, cols],
-                                    rhs=w_codes["out", hh][:].bitcast(E4), rhs_scale=w_scales["out", hh][:],
-                                    start=(hh == 0), stop=(hh == 1))
+        def second_stage(pair, half):
+            for row in (2 * pair, 2 * pair + 1):
+                if half == 0:
+                    y_acc[row] = psum.tile([P, OUT], F32, name="y%d" % row, tag="bank")
+                q = chunk_of_row[row]
+                h_codes, h_scales = h_mx[2 * q + half]
+                w_codes, w_scales = w_mx["out", half]
+                cols = slice(P * (row - CHUNKS[q][0]), P * (row - CHUNKS[q][0]) + P)
+                nc.tensor.matmul_mx(
+                    out=y_acc[row][:], lhsT=h_codes[:, cols].bitcast(E5M2), lhsT_scale=h_scales[:, cols],
+                    rhs=w_codes[:].bitcast(E4M3), rhs_scale=w_scales[:], start=(half == 0), stop=(half == 1),
+                )
 
-        def y_bias(r, lo=0, hi=PO):
-            pair = r // 2
+        def y_bias(pair, c0, c1):
             if pair not in y_sb:
-                y_sb[pair] = keep.tile([P, 2, PO], F32, name="ysb%d" % pair)
-            nc.vector.tensor_tensor(out=y_sb[pair][:, r % 2, lo:hi], in0=y_acc[r][:, lo:hi], in1=bias_out[:, lo:hi], op=ALU.add)
+                y_sb[pair] = keep.tile([P, 2, OUT], F32, name="y_sb%d" % pair)
+            for j in range(2):
+                nc.vector.tensor_tensor(
+                    out=y_sb[pair][:, j, c0:c1], in0=y_acc[2 * pair + j][:, c0:c1], in1=bias_out[:, c0:c1], op=ALU.add
+                )
 
-        def y_tanh(pair, r0=0, r1=2):
-            mat = work.tile([P, r1 - r0, S], F32, name="mat%d_%d" % (pair, r0), tag="mat", bufs=3)
-            nc.scalar.activation(out=mat[:], in_=y_sb[pair][:, r0:r1, 0:S], func=ACT.Tanh)
-            nc.sync.dma_start(out=material_v[:, 2 * pair + r0 : 2 * pair + r1, :], in_=mat[:])
+        def material_out(pair, j0=0, j1=2):
+            planes = work.tile([P, j1 - j0, PLANES], F32, name="planes%d_%d" % (pair, j0), tag="planes", bufs=3)
+            nc.scalar.activation(out=planes[:], in_=y_sb[pair][:, j0:j1, 0:PLANES], func=ACT.Tanh)
+            nc.sync.dma_start(out=material_rows[:, 2 * pair + j0 : 2 * pair + j1, :], in_=planes[:])
 
-        slope_sq = {}
-
-        def slope_square(pair):
-            t = work.tile([P, 2, 2 * D], F32, name="ssq%d" % pair, tag="slope_sq", bufs=2)
-            slope_sq[pair] = t
-            s = y_sb[pair][:, :, S:PO]
-            if SQ_ENG[pair] == "S":
-                nc.scalar.activation(out=t[:], in_=s, func=ACT.Square)
+        def slope_square(pair, engine):
+            slope_squares[pair] = work.tile([P, 2, 2 * SUB], F32, name="slope_squares%d" % pair, tag="slope_squares")
+            slopes = y_sb[pair][:, :, PLANES:OUT]
+            if engine == "scalar":
+                nc.scalar.activation(out=slope_squares[pair][:], in_=slopes, func=ACT.Square)
             else:
-                (nc.vector if SQ_ENG[pair] == "V" else nc.gpsimd).tensor_tensor(out=t[:], in0=s, in1=s, op=ALU.mult)
+                nc.vector.tensor_tensor(out=slope_squares[pair][:], in0=slopes, in1=slopes, op=ALU.mult)
 
-        sums = keep.tile([P, 16, D], F32, name="sums")
+        def slope_sum(pair):
+            both = slope_squares[pair]
+            nc.vector.tensor_tensor(
+                out=slope_sums[:, 2 * pair : 2 * pair + 2, :], in0=both[:, :, 0:SUB], in1=both[:, :, SUB : 2 * SUB], op=ALU.add
+            )
 
-        def slope_add(pair):
-            t = slope_sq[pair]
-            (nc.vector if SUM_ENG[pair] == "V" else nc.gpsimd).tensor_tensor(
-                out=sums[:, 2 * pair : 2 * pair + 2, :], in0=t[:, :, 0:D], in1=t[:, :, D : 2 * D], op=ALU.add)
+        def inverse_root(pair0, pair1):
+            rows = slice(2 * pair0, 2 * pair1)
+            nc.scalar.activation(
+                out=normals[:, rows, 2 * SUB : 3 * SUB], in_=slope_sums[:, rows, :], func=ACT.Abs_reciprocal_sqrt, bias=one[:]
+            )
 
-        normals = keep.tile([P, 16, 3 * D], F32, name="normals")
+        def normal_out(pair0):
+            for pair in (pair0, pair0 + 1):
+                rows = slice(2 * pair, 2 * pair + 2)
+                nc.vector.tensor_tensor(
+                    out=normals[:, rows, 0 : 2 * SUB].rearrange("p r (a d) -> p r a d", a=2),
+                    in0=y_sb[pair][:, :, PLANES:OUT].rearrange("p r (a d) -> p r a d", a=2),
+                    in1=normals[:, rows, 2 * SUB : 3 * SUB].unsqueeze(2).to_broadcast([P, 2, 2, SUB]),
+                    op=ALU.mult,
+                )
+            rows = slice(2 * pair0, 2 * pair0 + 4)
+            nc.sync.dma_start(out=normal_rows[:, rows, :], in_=normals[:, rows, :])
 
-        def inverse_root(p0, p1):
-            nc.scalar.activation(out=normals[:, 2 * p0 : 2 * p1, 2 * D : 3 * D], in_=sums[:, 2 * p0 : 2 * p1, :],
-                                 func=ACT.Abs_reciprocal_sqrt, bias=1.0)
-
-        def normal_out(pair, store):
-            rows = slice(2 * pair, 2 * pair + 2)
-            eng = nc.vector if MUL_ENG[pair // 2] == "V" else nc.gpsimd
-            eng.tensor_tensor(
-                out=normals[:, rows, 0 : 2 * D].rearrange("p r (a d) -> p r a d", a=2),
-                in0=y_sb[pair][:, :, S:PO].rearrange("p r (a d) -> p r a d", a=2),
-                in1=normals[:, rows, 2 * D : 3 * D].unsqueeze(2).to_broadcast([P, 2, 2, D]), op=ALU.mult)
-            if store:
-                rows = slice(2 * (pair + 1 - store), 2 * pair + 2)
-                nc.sync.dma_start(out=normal_v[:, rows, :], in_=normals[:, rows, :])
-
-        for r in range(4):
-            x_coarse(r)
-        w_interleave(0, 0)
-        w_interleave(0, 1)
+        for row in range(4):
+            x_coarse(row)
+        weight_interleave("win", 0, 0, "scalar")
+        weight_interleave("win", 0, 1, "scalar")
         x_blend(0)
         x_blend(1)
         x_transpose(0)
         x_blend(2)
         x_blend(3)
-        x_copy(0)
+        x_copy(0, "vector")
         x_transpose(1)
-        w_quantize(0)
-        nc.vector.tensor_copy(out=win_scale[:], in_=width_bf)
-        nc.vector.tensor_tensor(out=win_bias[:], in0=width_bf, in1=center_bf, op=ALU.mult)
+        weight_quantize("win", 0)
+        nc.vector.tensor_copy(out=window_scale[:], in_=width_bf)
+        nc.vector.tensor_tensor(out=window_bias[:], in0=width_bf, in1=center_bf, op=ALU.mult)
         x_coarse(4)
-        x_copy(1)
-        w_interleave(1, 0)
-        w_interleave(1, 1)
+        x_copy(1, "vector")
+        weight_interleave("car", 0, 0, "scalar")
+        weight_interleave("car", 0, 1, "scalar")
         x_coarse(5)
         x_quantize(0)
-        w_interleave(2, 0)
+        weight_interleave("win", 1, 0, "scalar")
         window_square(0, 0)
         window_square(0, 1)
         x_blend(4)
         x_blend(5)
         x_coarse(6)
         x_coarse(7)
-        w_quantize(1)
+        weight_quantize("car", 0)
         window_square(0, 2)
         window_square(0, 3)
         x_transpose(2)
-        w_interleave(2, 1)
+        weight_interleave("win", 1, 1, "vector")
         x_blend(6)
         x_blend(7)
-        x_copy(2)
-        window_exp(0, 0, 4)
-        w_quantize(2)
+        x_copy(2, "scalar")
+        window_exp(0)
+        weight_quantize("win", 1)
         x_coarse(8)
         x_coarse(9)
-        w_interleave(3, 0)
-        w_interleave(3, 1)
-        w_interleave(4, 0)
+        weight_interleave("car", 1, 0, "vector")
+        weight_interleave("car", 1, 1, "vector")
+        weight_interleave("out", 0, 0, "vector")
         window_square(1, 0)
         window_square(1, 1)
 
-        last = len(steps) - 1
-        y_due = {2: 0, 3: 1, 4: 2, 5: 3, 6: 4, 7: 5, 8: 6}
-        blend_due = {it: pair for pair, it in BLEND_AT.items()}
-        blend_due[-1] = 3
+        blend_round = {-1: 3, 0: 4, 1: 5, 3: 6, 4: 7}
+        y_from = 2
+        gpsimd_share = {}
         for i in range(last):
-            pair_h = blend_due.get(i - 1)
-            pair_y = y_due.get(i)
-            pair_x = blend_due.get(i)
-            pair_f = blend_due.get(i + 1)
-            pair_t = y_due.get(i - 1)
+            y_pair = i - y_from if i >= y_from else None
+            done_pair = i - 1 - y_from if i > y_from else None
+            turn_pair = blend_round.get(i - 1)
+            blend_pair = blend_round.get(i)
+            next_pair = blend_round.get(i + 1)
+
             carrier(i, 0)
             carrier(i, 1)
-            if pair_h is not None:
-                x_transpose(pair_h)
-                x_copy(pair_h)
+            if turn_pair is not None:
+                x_transpose(turn_pair)
+                x_copy(turn_pair, "scalar")
             carrier(i, 2)
             window_square(i + 1, 2)
             window_square(i + 1, 3)
-            acc_last = stage1("car", i, 3, "v", V_BUFS)
-            if i > 0 and D_REST[i - 1] == "V":
-                h_interleave_rest(i - 1)
-            if pair_t is not None and SQ_ENG[pair_t] != "S":
-                slope_square(pair_t)
-            if pair_f is not None:
-                x_coarse(2 * pair_f)
+            last_carrier = first_stage("car", i, 3)
+
+            if 0 < i <= SCALAR_REST_FROM:
+                h_interleave(i - 1, "vector", gpsimd_share[i - 1], texels[i - 1])
+            if done_pair is not None:
+                slope_square(done_pair, "vector")
+            if next_pair is not None:
+                x_coarse(2 * next_pair)
             if i == 0:
-                w_quantize(3)
-            if i == 2:
-                w_quantize(4)
-                w_quantize(5)
-            if pair_y is not None:
-                y_matmul(2 * pair_y, 0, 1)
-                y_matmul(2 * pair_y + 1, 0, 1)
+                weight_quantize("car", 1)
+            if i == y_from:
+                weight_quantize("out", 0)
+                weight_quantize("out", 1)
+            if y_pair is not None:
+                second_stage(y_pair, 0)
             if i > 0:
                 h_quantize(i - 1)
             if i % 2 == 0 and i // 2 + 1 < len(CHUNKS):
                 x_quantize(i // 2 + 1)
-            if pair_y is not None:
-                y_matmul(2 * pair_y, 1, 2)
-                y_matmul(2 * pair_y + 1, 1, 2)
-            if pair_t is not None:
-                y_tanh(pair_t)
-            if pair_t is not None and SQ_ENG[pair_t] == "S":
-                slope_square(pair_t)
-            if i == M4B:
-                w_interleave(4, 1)
-            window_exp(i + 1, 0, 4)
-            if pair_x is not None:
-                x_blend(2 * pair_x)
-                x_blend(2 * pair_x + 1)
+            if y_pair is not None:
+                second_stage(y_pair, 1)
+            if done_pair is not None:
+                material_out(done_pair)
+            if i == 0:
+                weight_interleave("out", 0, 1, "scalar")
+            window_exp(i + 1)
+            if blend_pair is not None:
+                x_blend(2 * blend_pair)
+                x_blend(2 * blend_pair + 1)
             if i == 1:
-                w_interleave(5, 0)
-                w_interleave(5, 1)
-            if pair_f is not None:
-                x_coarse(2 * pair_f + 1)
-            if pair_t is not None:
-                slope_add(pair_t)
-            carrier(i, 3, acc_last)
-            h_interleave(i)
+                weight_interleave("out", 1, 0, "scalar")
+                weight_interleave("out", 1, 1, "vector")
+            if next_pair is not None:
+                x_coarse(2 * next_pair + 1)
+            if done_pair is not None:
+                slope_sum(done_pair)
+
+            h_product(i, 3, last_carrier)
+            psum_columns = (2 * OUT if y_pair is not None else 0) + (3 if i + 1 < last else 4) * texels[i + 1]
+            share = int((psum_columns - GPSIMD_LEAD) * GPSIMD_RATE) // 32 * 32
+            gpsimd_share[i] = min(share, texels[i])
+            h_interleave(i, "gpsimd", 0, gpsimd_share[i])
             if i + 2 <= last:
                 window_square(i + 2, 0)
                 window_square(i + 2, 1)
-            if D_REST[i] == "S":
-                h_interleave_rest(i)
-            if pair_y is not None:
-                y_bias(2 * pair_y)
-                y_bias(2 * pair_y + 1)
+            if i >= SCALAR_REST_FROM and gpsimd_share[i] < texels[i]:
+                h_interleave(i, "scalar", gpsimd_share[i], texels[i])
+            if y_pair is not None:
+                y_bias(y_pair, 0, OUT)
 
-        y_tanh(6)
-        for t in range(4):
+        final = PAIRS - 1
+        material_out(final - 1)
+        for t in range(SLOTS):
             carrier(last, t)
         h_quantize(last - 1)
-        y_matmul(14, 0, 1)
-        y_matmul(15, 0, 1)
-        h_interleave(last)
+        second_stage(final, 0)
+        h_interleave(last, "vector", 0, texels[last])
         inverse_root(0, 2)
         inverse_root(2, 4)
-        slope_square(6)
+        slope_square(final - 1, "scalar")
         h_quantize(last)
-        y_matmul(14, 1, 2)
-        y_matmul(15, 1, 2)
-        normal_out(0, 0)
-        normal_out(1, 2)
-        slope_add(6)
-        inverse_root(4, 7)
-        y_bias(14, S, PO)
-        y_bias(15, S, PO)
-        slope_square(7)
-        normal_out(2, 0)
-        normal_out(3, 2)
-        slope_add(7)
-        inverse_root(7, 8)
-        y_bias(14, 0, S)
-        y_bias(15, 0, S)
-        for pair in range(4, 8):
-            normal_out(pair, 2 if pair % 2 == 1 else 0)
-        y_tanh(7, 0, 1)
-        y_tanh(7, 1, 2)
+        second_stage(final, 1)
+        normal_out(0)
+        slope_sum(final - 1)
+        inverse_root(4, final)
+        y_bias(final, PLANES, OUT)
+        slope_square(final, "scalar")
+        normal_out(2)
+        slope_sum(final)
+        inverse_root(final, PAIRS)
+        y_bias(final, 0, PLANES)
+        normal_out(4)
+        normal_out(6)
+        material_out(final, 0, 1)
+        material_out(final, 1, 2)

@@ -22,9 +22,9 @@ ROWS = M // P
 PAIRS = ROWS // 2
 PART = 256
 CHUNKS = [(0, 4), (4, 4), (8, 4), (12, 2), (14, 2)]
-GPSIMD_RATE = 3 / 16
+GPSIMD_RATE = 5 / 16
 GPSIMD_LEAD = 512
-SCALAR_REST_FROM = 4
+SHARE_STEP = 32
 
 
 def tile_windowed_texture_decoder_f3_kernel(
@@ -71,7 +71,7 @@ def tile_windowed_texture_decoder_f3_kernel(
 
         def load_hidden_vector(vec, name):
             tile = keep.tile([P, 2, SLOTS], BF16, name=name)
-            nc.gpsimd.dma_start(out=tile[:], in_=vec.rearrange("(h p t) -> p h t", h=2, t=SLOTS))
+            nc.sync.dma_start(out=tile[:], in_=vec.rearrange("(h p t) -> p h t", h=2, t=SLOTS))
             return tile[:].rearrange("p h t -> p (h t)")
 
         lod_bf = keep.tile([P, ROWS], BF16, name="lod_bf")
@@ -82,31 +82,29 @@ def tile_windowed_texture_decoder_f3_kernel(
         load_weight("win", 0, (1,))
         load_fine(1)
         load_weight("car", 0)
-        load_coarse(1)
-        load_fine(2)
-        load_weight("win", 1)
-        load_fine(3)
-        load_weight("car", 1)
-        load_weight("out", 0)
-        load_weight("out", 1)
-        bias_out = keep.tile([P, OUT], BF16, name="bias_out")
-        nc.sync.dma_start(out=bias_out[:], in_=b_out.partition_broadcast(P))
-        for group in (2, 3):
-            load_coarse(group)
-            load_fine(2 * group)
-            load_fine(2 * group + 1)
         width_bf = load_hidden_vector(width, "width_bf")
         center_bf = load_hidden_vector(center, "center_bf")
+        load_coarse(1)
+        load_weight("win", 1)
+        load_fine(2)
+        load_fine(3)
         bias_car = load_hidden_vector(b_car, "bias_car")
+        load_weight("car", 1)
+        load_weight("out", 0)
+        load_coarse(2)
+        load_fine(4)
+        load_weight("out", 1)
+        load_fine(5)
+        load_coarse(3)
+        load_fine(6)
+        load_fine(7)
+        bias_out = keep.tile([P, OUT], BF16, name="bias_out")
+        nc.sync.dma_start(out=bias_out[:], in_=b_out.partition_broadcast(P))
 
         identity = keep.tile([P, P], F32, name="identity")
         make_identity(nc, identity[:])
-        coarse_share = keep.tile([P, ROWS], F32, name="coarse_share")
         fine_share = keep.tile([P, ROWS], F32, name="fine_share")
-        nc.vector.tensor_copy(out=coarse_share[:], in_=lod_bf[:])
-        nc.vector.tensor_scalar(
-            out=fine_share[:], in0=lod_bf[:], scalar1=-1.0, scalar2=1.0, op0=ALU.mult, op1=ALU.add
-        )
+        nc.scalar.activation(out=fine_share[:], in_=lod_bf[:], func=ACT.Identity, scale=-1.0, bias=one[:])
 
         def move(engine, out, in_):
             if engine == "vector":
@@ -153,16 +151,17 @@ def tile_windowed_texture_decoder_f3_kernel(
         def x_coarse(row):
             coarse_part[row] = work.tile([P, K], F32, name="coarse_part%d" % row, tag="coarse_part", bufs=4)
             nc.vector.tensor_scalar(
-                out=coarse_part[row][:], in0=coarse_sb[row // 4][:], scalar1=coarse_share[:, row : row + 1],
+                out=coarse_part[row][:], in0=coarse_sb[row // 4][:], scalar1=lod_bf[:, row : row + 1],
                 scalar2=None, op0=ALU.mult,
             )
 
-        def x_blend(row):
-            x_bf[row] = work.tile([P, K], BF16, name="x_bf%d" % row, tag="x_bf", bufs=4)
-            nc.vector.scalar_tensor_tensor(
-                out=x_bf[row][:], in0=fine_sb[row // 2][:, row % 2, :], scalar=fine_share[:, row : row + 1],
-                in1=coarse_part[row][:], op0=ALU.mult, op1=ALU.add,
-            )
+        def x_blend(pair):
+            for row in (2 * pair + 1, 2 * pair):
+                x_bf[row] = work.tile([P, K], BF16, name="x_bf%d" % row, tag="x_bf", bufs=4)
+                nc.vector.scalar_tensor_tensor(
+                    out=x_bf[row][:], in0=fine_sb[pair][:, row % 2, :], scalar=fine_share[:, row : row + 1],
+                    in1=coarse_part[row][:], op0=ALU.mult, op1=ALU.add,
+                )
 
         def x_transpose(pair):
             x_turned[pair] = psum.tile([P, 2, 2, P], F32, name="x_turned%d" % pair, tag="bank")
@@ -189,8 +188,11 @@ def tile_windowed_texture_decoder_f3_kernel(
         window_bias = keep.tile([P, 2 * SLOTS], F32, name="window_bias")
         squares, gauss, h_slots, h_grouped, h_mx = {}, {}, {}, {}, {}
 
+        first_acc = {}
+
         def first_stage(which, i, t):
             acc = psum.tile([P, texels[i]], F32, name="%s%d_%d" % (which, i, t), tag="bank")
+            first_acc[which, i, t] = acc
             w_codes, w_scales = w_mx[which, i % 2]
             x_codes, x_scales = x_mx[i // 2]
             cols = slice(P * t, P * t + P)
@@ -198,32 +200,28 @@ def tile_windowed_texture_decoder_f3_kernel(
                 out=acc[:], lhsT=w_codes[:, cols].bitcast(E4M3), lhsT_scale=w_scales[:, cols],
                 rhs=x_codes[:].bitcast(E4M3), rhs_scale=x_scales[:], start=True, stop=True,
             )
-            return acc
 
         def window_square(i, t):
             if t == 0:
                 squares[i] = work.tile([P, SLOTS, texels[i]], F32, name="squares%d" % i, tag="squares")
-            acc = first_stage("win", i, t)
+            acc = first_acc["win", i, t]
             col = slice(SLOTS * (i % 2) + t, SLOTS * (i % 2) + t + 1)
             nc.scalar.activation(
                 out=squares[i][:, t, :], in_=acc[:], func=ACT.Square, scale=window_scale[:, col], bias=window_bias[:, col]
             )
 
         def window_exp(i):
-            gauss[i] = work.tile([P, SLOTS, texels[i]], F32, name="gauss%d" % i, tag="gauss", bufs=3)
+            gauss[i] = work.tile([P, SLOTS, texels[i]], F32, name="gauss%d" % i, tag="gauss")
             nc.scalar.activation(out=gauss[i][:], in_=squares[i][:], func=ACT.Exp, scale=-0.5)
 
-        def h_product(i, t, acc):
+        def h_product(i, t):
             if t == 0:
                 h_slots[i] = work.tile([P, SLOTS, texels[i]], BF16, name="h_slots%d" % i, tag="h_slots", bufs=3)
             col = slice(SLOTS * (i % 2) + t, SLOTS * (i % 2) + t + 1)
             nc.vector.scalar_tensor_tensor(
-                out=h_slots[i][:, t, :], in0=acc[:], scalar=bias_car[:, col], in1=gauss[i][:, t, :],
+                out=h_slots[i][:, t, :], in0=first_acc["car", i, t][:], scalar=bias_car[:, col], in1=gauss[i][:, t, :],
                 op0=ALU.add, op1=ALU.mult,
             )
-
-        def carrier(i, t):
-            h_product(i, t, first_stage("car", i, t))
 
         def h_interleave(i, engine, c0, c1):
             if c0 == 0:
@@ -233,12 +231,13 @@ def tile_windowed_texture_decoder_f3_kernel(
         def h_quantize(i):
             h_mx[i] = quantize(h_grouped[i][:].rearrange("p c t -> p (c t)"), E5M2, work, "h%d" % i, tag="h", bufs=4)
 
-        y_acc, y_sb, slope_squares = {}, {}, {}
+        y_acc, slope_squares = {}, {}
+        y_sb = keep.tile([P, ROWS, OUT], F32, name="y_sb")
         slope_sums = keep.tile([P, ROWS, SUB], F32, name="slope_sums")
         normals = keep.tile([P, ROWS, 3 * SUB], F32, name="normals")
 
         def second_stage(pair, half):
-            for row in (2 * pair, 2 * pair + 1):
+            for row in (2 * pair + half, 2 * pair + 1 - half):
                 if half == 0:
                     y_acc[row] = psum.tile([P, OUT], F32, name="y%d" % row, tag="bank")
                 q = chunk_of_row[row]
@@ -251,30 +250,29 @@ def tile_windowed_texture_decoder_f3_kernel(
                 )
 
         def y_bias(pair, c0, c1):
-            if pair not in y_sb:
-                y_sb[pair] = keep.tile([P, 2, OUT], F32, name="y_sb%d" % pair)
             for j in range(2):
                 nc.vector.tensor_tensor(
-                    out=y_sb[pair][:, j, c0:c1], in0=y_acc[2 * pair + j][:, c0:c1], in1=bias_out[:, c0:c1], op=ALU.add
+                    out=y_sb[:, 2 * pair + j, c0:c1], in0=y_acc[2 * pair + j][:, c0:c1], in1=bias_out[:, c0:c1], op=ALU.add
                 )
 
         def material_out(pair, j0=0, j1=2):
-            planes = work.tile([P, j1 - j0, PLANES], F32, name="planes%d_%d" % (pair, j0), tag="planes", bufs=3)
-            nc.scalar.activation(out=planes[:], in_=y_sb[pair][:, j0:j1, 0:PLANES], func=ACT.Tanh)
+            planes = work.tile([P, j1 - j0, PLANES], F32, name="planes%d_%d" % (pair, j0), tag="planes", bufs=4)
+            nc.scalar.activation(out=planes[:], in_=y_sb[:, 2 * pair + j0 : 2 * pair + j1, 0:PLANES], func=ACT.Tanh)
             nc.sync.dma_start(out=material_rows[:, 2 * pair + j0 : 2 * pair + j1, :], in_=planes[:])
 
-        def slope_square(pair, engine):
-            slope_squares[pair] = work.tile([P, 2, 2 * SUB], F32, name="slope_squares%d" % pair, tag="slope_squares")
-            slopes = y_sb[pair][:, :, PLANES:OUT]
+        def slope_square(pair0, pair1, engine):
+            slopes = y_sb[:, 2 * pair0 : 2 * pair1, PLANES:OUT]
+            both = work.tile([P, 2 * (pair1 - pair0), 2 * SUB], F32, name="slope_squares%d" % pair0, tag="slope_squares")
+            slope_squares[pair0] = both
             if engine == "scalar":
-                nc.scalar.activation(out=slope_squares[pair][:], in_=slopes, func=ACT.Square)
+                nc.scalar.activation(out=both[:], in_=slopes, func=ACT.Square)
             else:
-                nc.vector.tensor_tensor(out=slope_squares[pair][:], in0=slopes, in1=slopes, op=ALU.mult)
+                nc.vector.tensor_tensor(out=both[:], in0=slopes, in1=slopes, op=ALU.mult)
 
-        def slope_sum(pair):
-            both = slope_squares[pair]
+        def slope_sum(pair0, pair1):
+            both = slope_squares[pair0]
             nc.vector.tensor_tensor(
-                out=slope_sums[:, 2 * pair : 2 * pair + 2, :], in0=both[:, :, 0:SUB], in1=both[:, :, SUB : 2 * SUB], op=ALU.add
+                out=slope_sums[:, 2 * pair0 : 2 * pair1, :], in0=both[:, :, 0:SUB], in1=both[:, :, SUB : 2 * SUB], op=ALU.add
             )
 
         def inverse_root(pair0, pair1):
@@ -283,16 +281,14 @@ def tile_windowed_texture_decoder_f3_kernel(
                 out=normals[:, rows, 2 * SUB : 3 * SUB], in_=slope_sums[:, rows, :], func=ACT.Abs_reciprocal_sqrt, bias=one[:]
             )
 
-        def normal_out(pair0):
-            for pair in (pair0, pair0 + 1):
-                rows = slice(2 * pair, 2 * pair + 2)
-                nc.vector.tensor_tensor(
-                    out=normals[:, rows, 0 : 2 * SUB].rearrange("p r (a d) -> p r a d", a=2),
-                    in0=y_sb[pair][:, :, PLANES:OUT].rearrange("p r (a d) -> p r a d", a=2),
-                    in1=normals[:, rows, 2 * SUB : 3 * SUB].unsqueeze(2).to_broadcast([P, 2, 2, SUB]),
-                    op=ALU.mult,
-                )
-            rows = slice(2 * pair0, 2 * pair0 + 4)
+        def normal_out(pair0, pair1):
+            rows = slice(2 * pair0, 2 * pair1)
+            nc.vector.tensor_tensor(
+                out=normals[:, rows, 0 : 2 * SUB].rearrange("p r (a d) -> p r a d", a=2),
+                in0=y_sb[:, rows, PLANES:OUT].rearrange("p r (a d) -> p r a d", a=2),
+                in1=normals[:, rows, 2 * SUB : 3 * SUB].unsqueeze(2).to_broadcast([P, 2 * (pair1 - pair0), 2, SUB]),
+                op=ALU.mult,
+            )
             nc.sync.dma_start(out=normal_rows[:, rows, :], in_=normals[:, rows, :])
 
         for row in range(4):
@@ -300,26 +296,25 @@ def tile_windowed_texture_decoder_f3_kernel(
         weight_interleave("win", 0, 0, "scalar")
         weight_interleave("win", 0, 1, "scalar")
         x_blend(0)
-        x_blend(1)
         x_transpose(0)
-        x_blend(2)
-        x_blend(3)
-        x_copy(0, "vector")
+        x_blend(1)
         x_transpose(1)
+        x_copy(0, "vector")
         weight_quantize("win", 0)
-        nc.vector.tensor_copy(out=window_scale[:], in_=width_bf)
-        nc.vector.tensor_tensor(out=window_bias[:], in0=width_bf, in1=center_bf, op=ALU.mult)
         x_coarse(4)
         x_copy(1, "vector")
+        move("gpsimd", window_scale[:], width_bf)
+        nc.gpsimd.tensor_tensor(out=window_bias[:], in0=width_bf, in1=center_bf, op=ALU.mult)
         weight_interleave("car", 0, 0, "scalar")
         weight_interleave("car", 0, 1, "scalar")
         x_coarse(5)
         x_quantize(0)
         weight_interleave("win", 1, 0, "scalar")
+        for t in range(SLOTS):
+            first_stage("win", 0, t)
         window_square(0, 0)
         window_square(0, 1)
-        x_blend(4)
-        x_blend(5)
+        x_blend(2)
         x_coarse(6)
         x_coarse(7)
         weight_quantize("car", 0)
@@ -327,16 +322,19 @@ def tile_windowed_texture_decoder_f3_kernel(
         window_square(0, 3)
         x_transpose(2)
         weight_interleave("win", 1, 1, "vector")
-        x_blend(6)
-        x_blend(7)
+        x_blend(3)
         x_copy(2, "scalar")
         window_exp(0)
         weight_quantize("win", 1)
+        first_stage("car", 0, 1)
+        first_stage("car", 0, 0)
         x_coarse(8)
         x_coarse(9)
         weight_interleave("car", 1, 0, "vector")
         weight_interleave("car", 1, 1, "vector")
         weight_interleave("out", 0, 0, "vector")
+        first_stage("win", 1, 1)
+        first_stage("win", 1, 0)
         window_square(1, 0)
         window_square(1, 1)
 
@@ -349,21 +347,25 @@ def tile_windowed_texture_decoder_f3_kernel(
             turn_pair = blend_round.get(i - 1)
             blend_pair = blend_round.get(i)
             next_pair = blend_round.get(i + 1)
+            slopes_due = done_pair is not None and done_pair % 2 == 1
+            square_engine = "vector" if i == last - 1 else "scalar"
 
-            carrier(i, 0)
-            carrier(i, 1)
+            h_product(i, 0)
+            h_product(i, 1)
             if turn_pair is not None:
                 x_transpose(turn_pair)
+            first_stage("car", i, 2)
+            h_product(i, 2)
+            first_stage("win", i + 1, 3)
+            first_stage("win", i + 1, 2)
+            if turn_pair is not None:
                 x_copy(turn_pair, "scalar")
-            carrier(i, 2)
             window_square(i + 1, 2)
             window_square(i + 1, 3)
-            last_carrier = first_stage("car", i, 3)
+            first_stage("car", i, 3)
 
-            if 0 < i <= SCALAR_REST_FROM:
+            if i > 0 and gpsimd_share[i - 1] < texels[i - 1]:
                 h_interleave(i - 1, "vector", gpsimd_share[i - 1], texels[i - 1])
-            if done_pair is not None:
-                slope_square(done_pair, "vector")
             if next_pair is not None:
                 x_coarse(2 * next_pair)
             if i == 0:
@@ -377,59 +379,67 @@ def tile_windowed_texture_decoder_f3_kernel(
                 h_quantize(i - 1)
             if i % 2 == 0 and i // 2 + 1 < len(CHUNKS):
                 x_quantize(i // 2 + 1)
+            first_stage("car", i + 1, 1)
+            first_stage("car", i + 1, 0)
             if y_pair is not None:
                 second_stage(y_pair, 1)
             if done_pair is not None:
                 material_out(done_pair)
+            if slopes_due and square_engine == "scalar":
+                slope_square(done_pair - 1, done_pair + 1, "scalar")
             if i == 0:
                 weight_interleave("out", 0, 1, "scalar")
             window_exp(i + 1)
             if blend_pair is not None:
-                x_blend(2 * blend_pair)
-                x_blend(2 * blend_pair + 1)
+                x_blend(blend_pair)
             if i == 1:
                 weight_interleave("out", 1, 0, "scalar")
                 weight_interleave("out", 1, 1, "vector")
             if next_pair is not None:
                 x_coarse(2 * next_pair + 1)
-            if done_pair is not None:
-                slope_sum(done_pair)
+            if slopes_due and square_engine == "vector":
+                slope_square(done_pair - 1, done_pair + 1, "vector")
+            h_product(i, 3)
+            if slopes_due:
+                slope_sum(done_pair - 1, done_pair + 1)
 
-            h_product(i, 3, last_carrier)
-            psum_columns = (2 * OUT if y_pair is not None else 0) + (3 if i + 1 < last else 4) * texels[i + 1]
-            share = int((psum_columns - GPSIMD_LEAD) * GPSIMD_RATE) // 32 * 32
+            psum_columns = (2 * OUT if y_pair is not None else 0) + (3 if i + 1 < last else SLOTS) * texels[i + 1]
+            share = int((psum_columns - GPSIMD_LEAD) * GPSIMD_RATE) // SHARE_STEP * SHARE_STEP
             gpsimd_share[i] = min(share, texels[i])
             h_interleave(i, "gpsimd", 0, gpsimd_share[i])
             if i + 2 <= last:
+                first_stage("win", i + 2, 1)
+                first_stage("win", i + 2, 0)
                 window_square(i + 2, 0)
                 window_square(i + 2, 1)
-            if i >= SCALAR_REST_FROM and gpsimd_share[i] < texels[i]:
-                h_interleave(i, "scalar", gpsimd_share[i], texels[i])
             if y_pair is not None:
                 y_bias(y_pair, 0, OUT)
+        assert gpsimd_share[last - 1] == texels[last - 1]
 
         final = PAIRS - 1
+        first_stage("car", last, 3)
+        first_stage("car", last, 2)
         material_out(final - 1)
         for t in range(SLOTS):
-            carrier(last, t)
+            h_product(last, t)
         h_quantize(last - 1)
         second_stage(final, 0)
         h_interleave(last, "vector", 0, texels[last])
         inverse_root(0, 2)
         inverse_root(2, 4)
-        slope_square(final - 1, "scalar")
+        slope_square(final - 1, final, "scalar")
         h_quantize(last)
         second_stage(final, 1)
-        normal_out(0)
-        slope_sum(final - 1)
+        normal_out(0, 2)
+        slope_sum(final - 1, final)
         inverse_root(4, final)
         y_bias(final, PLANES, OUT)
-        slope_square(final, "scalar")
-        normal_out(2)
-        slope_sum(final)
+        slope_square(final, PAIRS, "scalar")
+        normal_out(2, 4)
+        slope_sum(final, PAIRS)
         inverse_root(final, PAIRS)
         y_bias(final, 0, PLANES)
-        normal_out(4)
-        normal_out(6)
+        normal_out(4, 6)
+        normal_out(6, PAIRS)
         material_out(final, 0, 1)
         material_out(final, 1, 2)

from contextlib import ExitStack

import concourse.mybir as mybir
from concourse.masks import make_identity

M, K, N, OUT, PLANES, SUB = 2048, 512, 1024, 512, 384, 64
FLOPS = 2 * M * K * N * 2 + 2 * M * N * OUT

F32 = mybir.dt.float32
BF16 = mybir.dt.bfloat16
U32 = mybir.dt.uint32
U8 = mybir.dt.uint8
E4M3 = mybir.dt.float8_e4m3fn_x4
E5M2 = mybir.dt.float8_e5m2_x4
ALU = mybir.AluOpType
ACT = mybir.ActivationFunctionType

P = 128
SLOTS = 4
PASS = P * SLOTS
ROWS = M // P
PAIRS = ROWS // 2
PART = 256
CHUNKS = [(0, 4), (4, 4), (8, 4), (12, 2), (14, 2)]
GPSIMD_RATE = 5 / 16
GPSIMD_LEAD = 512
SHARE_STEP = 32


def tile_windowed_texture_decoder_f3_kernel(
    tc, fine, coarse, lod, w_win, center, width, w_car, b_car, w_out, b_out, material, normal
):
    nc = tc.nc
    with ExitStack() as ctx:
        keep = ctx.enter_context(tc.tile_pool(name="keep", bufs=1))
        work = ctx.enter_context(tc.tile_pool(name="work", bufs=2))
        psum = ctx.enter_context(tc.psum_pool(name="psum", bufs=8))
        ctx.enter_context(tc.manual_schedule())

        fine_rows = fine.rearrange("(p r) k -> p r k", r=ROWS)
        coarse_rows = coarse.rearrange("(p g) k -> p g k", g=ROWS // 4)
        material_rows = material.rearrange("(p r) s -> p r s", r=ROWS)
        normal_rows = normal.rearrange("(p r) s -> p r s", r=ROWS)

        zero = keep.tile([P, 1], F32, name="zero")
        one = keep.tile([P, 1], F32, name="one")
        nc.vector.memset(zero[:], 0.0)
        nc.scalar.activation(out=one[:], in_=zero[:], func=ACT.Exp)

        coarse_sb, fine_sb, w_raw = {}, {}, {}

        def load_coarse(group):
            coarse_sb[group] = keep.tile([P, K], BF16, name="coarse%d" % group)
            nc.sync.dma_start(out=coarse_sb[group][:], in_=coarse_rows[:, group, :])

        def load_fine(pair):
            fine_sb[pair] = keep.tile([P, 2, K], BF16, name="fine%d" % pair)
            nc.sync.dma_start(out=fine_sb[pair][:], in_=fine_rows[:, 2 * pair : 2 * pair + 2, :])

        def load_weight(which, half, parts=(0, 1)):
            cols = PART * len(parts)
            raw = keep.tile([P, SLOTS, cols], BF16, name="raw_%s%d_%d" % (which, half, parts[0]))
            for n, part in enumerate(parts):
                w_raw[which, half, part] = raw[:, :, PART * n : PART * n + PART]
            if which == "out":
                src = w_out[PASS * half : PASS * half + PASS, :]
            else:
                first = PASS * half + PART * parts[0]
                src = (w_win if which == "win" else w_car)[:, first : first + cols]
            nc.sync.dma_start(out=raw[:], in_=src.rearrange("(p t) n -> p t n", t=SLOTS))

        def load_hidden_vector(vec, name):
            tile = keep.tile([P, 2, SLOTS], BF16, name=name)
            nc.sync.dma_start(out=tile[:], in_=vec.rearrange("(h p t) -> p h t", h=2, t=SLOTS))
            return tile[:].rearrange("p h t -> p (h t)")

        lod_bf = keep.tile([P, ROWS], BF16, name="lod_bf")
        nc.sync.dma_start(out=lod_bf[:], in_=lod.rearrange("(p r) -> p r", r=ROWS))
        load_coarse(0)
        load_weight("win", 0, (0,))
        load_fine(0)
        load_weight("win", 0, (1,))
        load_fine(1)
        load_weight("car", 0)
        width_bf = load_hidden_vector(width, "width_bf")
        center_bf = load_hidden_vector(center, "center_bf")
        load_coarse(1)
        load_weight("win", 1)
        load_fine(2)
        load_fine(3)
        bias_car = load_hidden_vector(b_car, "bias_car")
        load_weight("car", 1)
        load_weight("out", 0)
        load_coarse(2)
        load_fine(4)
        load_weight("out", 1)
        load_fine(5)
        load_coarse(3)
        load_fine(6)
        load_fine(7)
        bias_out = keep.tile([P, OUT], BF16, name="bias_out")
        nc.sync.dma_start(out=bias_out[:], in_=b_out.partition_broadcast(P))

        identity = keep.tile([P, P], F32, name="identity")
        make_identity(nc, identity[:])
        fine_share = keep.tile([P, ROWS], F32, name="fine_share")
        nc.scalar.activation(out=fine_share[:], in_=lod_bf[:], func=ACT.Identity, scale=-1.0, bias=one[:])

        def move(engine, out, in_):
            if engine == "vector":
                nc.vector.tensor_copy(out=out, in_=in_)
            elif engine == "scalar":
                nc.scalar.copy(out=out, in_=in_)
            else:
                nc.gpsimd.tensor_scalar(out=out, in0=in_, scalar1=1.0, scalar2=0.0, op0=ALU.mult, op1=ALU.add)

        def quantize(grouped, dtype, pool, name, tag="", bufs=None):
            cols = grouped.shape[1] // SLOTS
            codes = pool.tile([P, cols], U32, name=name + "_codes", tag=tag and tag + "_codes", bufs=bufs, align_bytes=64)
            scales = pool.tile([P, cols], U8, name=name + "_scales", tag=tag and tag + "_scales", bufs=bufs, align_bytes=64)
            nc.vector.quantize_mx(out=codes[:].bitcast(dtype), scales=scales[:], in_=grouped)
            return codes, scales

        w_grouped, w_mx = {}, {}

        def weight_interleave(which, half, part, engine):
            if part == 0:
                w_grouped[which, half] = work.tile(
                    [P, SLOTS * PASS], BF16, name="grouped_%s%d" % (which, half), tag="w_grouped", bufs=3, align_bytes=64
                )
            grouped = w_grouped[which, half][:]
            raw = w_raw[which, half, part]
            if which == "out":
                dst = grouped.rearrange("p (n t) -> p n t", t=SLOTS)[:, PART * part : PART * part + PART, :]
                move(engine, dst, raw.rearrange("p t n -> p n t"))
            else:
                m0 = PART // SLOTS * part
                dst = grouped.rearrange("p (s m t) -> p s m t", s=SLOTS, t=SLOTS)[:, :, m0 : m0 + PART // SLOTS, :]
                move(
                    engine,
                    dst.rearrange("p s (m i) t -> p m s i t", i=2),
                    raw.rearrange("p t (m i s) -> p m s i t", i=2, s=SLOTS),
                )

        def weight_quantize(which, half):
            w_mx[which, half] = quantize(w_grouped[which, half][:], E4M3, keep, "w_%s%d" % (which, half))

        coarse_part, x_bf, x_turned, x_grouped, x_mx = {}, {}, {}, {}, {}
        chunk_of_row = {r: q for q, (first, rows) in enumerate(CHUNKS) for r in range(first, first + rows)}

        def x_coarse(row):
            coarse_part[row] = work.tile([P, K], F32, name="coarse_part%d" % row, tag="coarse_part", bufs=4)
            nc.vector.tensor_scalar(
                out=coarse_part[row][:], in0=coarse_sb[row // 4][:], scalar1=lod_bf[:, row : row + 1],
                scalar2=None, op0=ALU.mult,
            )

        def x_blend(pair):
            for row in (2 * pair + 1, 2 * pair):
                x_bf[row] = work.tile([P, K], BF16, name="x_bf%d" % row, tag="x_bf", bufs=4)
                nc.vector.scalar_tensor_tensor(
                    out=x_bf[row][:], in0=fine_sb[pair][:, row % 2, :], scalar=fine_share[:, row : row + 1],
                    in1=coarse_part[row][:], op0=ALU.mult, op1=ALU.add,
                )

        def x_transpose(pair):
            x_turned[pair] = psum.tile([P, 2, 2, P], F32, name="x_turned%d" % pair, tag="bank")
            for j in range(2):
                words = x_bf[2 * pair + j][:].bitcast(F32)
                for u in range(2):
                    nc.tensor.transpose(x_turned[pair][:, j, u, :], words[:, u : K // 2 : 2], identity[:])

        def x_copy(pair, engine):
            q = chunk_of_row[2 * pair]
            first, rows = CHUNKS[q]
            if 2 * pair == first:
                x_grouped[q] = work.tile([P, 2 * P * rows], F32, name="x_grouped%d" % q, tag="x_grouped", align_bytes=64)
            w0 = 2 * P * (2 * pair - first)
            dst = x_grouped[q][:, w0 : w0 + 4 * P].rearrange("p (j c u) -> p j c u", j=2, u=2)
            move(engine, dst, x_turned[pair][:].rearrange("p j u c -> p j c u"))

        def x_quantize(q):
            x_mx[q] = quantize(x_grouped[q][:].bitcast(BF16), E4M3, keep, "x%d" % q)

        last = 2 * len(CHUNKS) - 1
        texels = [P * CHUNKS[i // 2][1] for i in range(last + 1)]
        window_scale = keep.tile([P, 2 * SLOTS], F32, name="window_scale")
        window_bias = keep.tile([P, 2 * SLOTS], F32, name="window_bias")
        squares, gauss, h_slots, h_grouped, h_mx = {}, {}, {}, {}, {}

        first_acc = {}

        def first_stage(which, i, t):
            acc = psum.tile([P, texels[i]], F32, name="%s%d_%d" % (which, i, t), tag="bank")
            first_acc[which, i, t] = acc
            w_codes, w_scales = w_mx[which, i % 2]
            x_codes, x_scales = x_mx[i // 2]
            cols = slice(P * t, P * t + P)
            nc.tensor.matmul_mx(
                out=acc[:], lhsT=w_codes[:, cols].bitcast(E4M3), lhsT_scale=w_scales[:, cols],
                rhs=x_codes[:].bitcast(E4M3), rhs_scale=x_scales[:], start=True, stop=True,
            )

        def window_square(i, t):
            if t == 0:
                squares[i] = work.tile([P, SLOTS, texels[i]], F32, name="squares%d" % i, tag="squares")
            acc = first_acc["win", i, t]
            col = slice(SLOTS * (i % 2) + t, SLOTS * (i % 2) + t + 1)
            nc.scalar.activation(
                out=squares[i][:, t, :], in_=acc[:], func=ACT.Square, scale=window_scale[:, col], bias=window_bias[:, col]
            )

        def window_exp(i):
            gauss[i] = work.tile([P, SLOTS, texels[i]], F32, name="gauss%d" % i, tag="gauss")
            nc.scalar.activation(out=gauss[i][:], in_=squares[i][:], func=ACT.Exp, scale=-0.5)

        def h_product(i, t):
            if t == 0:
                h_slots[i] = work.tile([P, SLOTS, texels[i]], BF16, name="h_slots%d" % i, tag="h_slots", bufs=3)
            col = slice(SLOTS * (i % 2) + t, SLOTS * (i % 2) + t + 1)
            nc.vector.scalar_tensor_tensor(
                out=h_slots[i][:, t, :], in0=first_acc["car", i, t][:], scalar=bias_car[:, col], in1=gauss[i][:, t, :],
                op0=ALU.add, op1=ALU.mult,
            )

        def h_interleave(i, engine, c0, c1):
            if c0 == 0:
                h_grouped[i] = work.tile([P, texels[i], SLOTS], BF16, name="h_grouped%d" % i, tag="h_grouped", align_bytes=64)
            move(engine, h_grouped[i][:, c0:c1, :], h_slots[i][:, :, c0:c1].rearrange("p t c -> p c t"))

        def h_quantize(i):
            h_mx[i] = quantize(h_grouped[i][:].rearrange("p c t -> p (c t)"), E5M2, work, "h%d" % i, tag="h", bufs=4)

        y_acc, slope_squares = {}, {}
        y_sb = keep.tile([P, ROWS, OUT], F32, name="y_sb")
        slope_sums = keep.tile([P, ROWS, SUB], F32, name="slope_sums")
        normals = keep.tile([P, ROWS, 3 * SUB], F32, name="normals")

        def second_stage(pair, half):
            for row in (2 * pair + half, 2 * pair + 1 - half):
                if half == 0:
                    y_acc[row] = psum.tile([P, OUT], F32, name="y%d" % row, tag="bank")
                q = chunk_of_row[row]
                h_codes, h_scales = h_mx[2 * q + half]
                w_codes, w_scales = w_mx["out", half]
                cols = slice(P * (row - CHUNKS[q][0]), P * (row - CHUNKS[q][0]) + P)
                nc.tensor.matmul_mx(
                    out=y_acc[row][:], lhsT=h_codes[:, cols].bitcast(E5M2), lhsT_scale=h_scales[:, cols],
                    rhs=w_codes[:].bitcast(E4M3), rhs_scale=w_scales[:], start=(half == 0), stop=(half == 1),
                )

        def y_bias(pair, c0, c1):
            for j in range(2):
                nc.vector.tensor_tensor(
                    out=y_sb[:, 2 * pair + j, c0:c1], in0=y_acc[2 * pair + j][:, c0:c1], in1=bias_out[:, c0:c1], op=ALU.add
                )

        def material_out(pair, j0=0, j1=2):
            planes = work.tile([P, j1 - j0, PLANES], F32, name="planes%d_%d" % (pair, j0), tag="planes", bufs=4)
            nc.scalar.activation(out=planes[:], in_=y_sb[:, 2 * pair + j0 : 2 * pair + j1, 0:PLANES], func=ACT.Tanh)
            nc.sync.dma_start(out=material_rows[:, 2 * pair + j0 : 2 * pair + j1, :], in_=planes[:])

        def slope_square(pair0, pair1, engine):
            slopes = y_sb[:, 2 * pair0 : 2 * pair1, PLANES:OUT]
            both = work.tile([P, 2 * (pair1 - pair0), 2 * SUB], F32, name="slope_squares%d" % pair0, tag="slope_squares")
            slope_squares[pair0] = both
            if engine == "scalar":
                nc.scalar.activation(out=both[:], in_=slopes, func=ACT.Square)
            else:
                nc.vector.tensor_tensor(out=both[:], in0=slopes, in1=slopes, op=ALU.mult)

        def slope_sum(pair0, pair1):
            both = slope_squares[pair0]
            nc.vector.tensor_tensor(
                out=slope_sums[:, 2 * pair0 : 2 * pair1, :], in0=both[:, :, 0:SUB], in1=both[:, :, SUB : 2 * SUB], op=ALU.add
            )

        def inverse_root(pair0, pair1):
            rows = slice(2 * pair0, 2 * pair1)
            nc.scalar.activation(
                out=normals[:, rows, 2 * SUB : 3 * SUB], in_=slope_sums[:, rows, :], func=ACT.Abs_reciprocal_sqrt, bias=one[:]
            )

        def normal_out(pair0, pair1):
            rows = slice(2 * pair0, 2 * pair1)
            nc.vector.tensor_tensor(
                out=normals[:, rows, 0 : 2 * SUB].rearrange("p r (a d) -> p r a d", a=2),
                in0=y_sb[:, rows, PLANES:OUT].rearrange("p r (a d) -> p r a d", a=2),
                in1=normals[:, rows, 2 * SUB : 3 * SUB].unsqueeze(2).to_broadcast([P, 2 * (pair1 - pair0), 2, SUB]),
                op=ALU.mult,
            )
            nc.sync.dma_start(out=normal_rows[:, rows, :], in_=normals[:, rows, :])

        for row in range(4):
            x_coarse(row)
        weight_interleave("win", 0, 0, "scalar")
        weight_interleave("win", 0, 1, "scalar")
        x_blend(0)
        x_transpose(0)
        x_blend(1)
        x_transpose(1)
        x_copy(0, "vector")
        weight_quantize("win", 0)
        x_coarse(4)
        x_copy(1, "vector")
        move("gpsimd", window_scale[:], width_bf)
        nc.gpsimd.tensor_tensor(out=window_bias[:], in0=width_bf, in1=center_bf, op=ALU.mult)
        weight_interleave("car", 0, 0, "scalar")
        weight_interleave("car", 0, 1, "scalar")
        x_coarse(5)
        x_quantize(0)
        weight_interleave("win", 1, 0, "scalar")
        for t in range(SLOTS):
            first_stage("win", 0, t)
        window_square(0, 0)
        window_square(0, 1)
        x_blend(2)
        x_coarse(6)
        x_coarse(7)
        weight_quantize("car", 0)
        window_square(0, 2)
        window_square(0, 3)
        x_transpose(2)
        weight_interleave("win", 1, 1, "vector")
        x_blend(3)
        x_copy(2, "scalar")
        window_exp(0)
        weight_quantize("win", 1)
        first_stage("car", 0, 1)
        first_stage("car", 0, 0)
        x_coarse(8)
        x_coarse(9)
        weight_interleave("car", 1, 0, "vector")
        weight_interleave("car", 1, 1, "vector")
        weight_interleave("out", 0, 0, "vector")
        first_stage("win", 1, 1)
        first_stage("win", 1, 0)
        window_square(1, 0)
        window_square(1, 1)

        blend_round = {-1: 3, 0: 4, 1: 5, 3: 6, 4: 7}
        y_from = 2
        gpsimd_share = {}
        for i in range(last):
            y_pair = i - y_from if i >= y_from else None
            done_pair = i - 1 - y_from if i > y_from else None
            turn_pair = blend_round.get(i - 1)
            blend_pair = blend_round.get(i)
            next_pair = blend_round.get(i + 1)
            slopes_due = done_pair is not None and done_pair % 2 == 1
            square_engine = "vector" if i == last - 1 else "scalar"

            h_product(i, 0)
            h_product(i, 1)
            if turn_pair is not None:
                x_transpose(turn_pair)
            first_stage("car", i, 2)
            h_product(i, 2)
            first_stage("win", i + 1, 3)
            first_stage("win", i + 1, 2)
            if turn_pair is not None:
                x_copy(turn_pair, "scalar")
            window_square(i + 1, 2)
            window_square(i + 1, 3)
            first_stage("car", i, 3)

            if i > 0 and gpsimd_share[i - 1] < texels[i - 1]:
                h_interleave(i - 1, "vector", gpsimd_share[i - 1], texels[i - 1])
            if next_pair is not None:
                x_coarse(2 * next_pair)
            if i == 0:
                weight_quantize("car", 1)
            if i == y_from:
                weight_quantize("out", 0)
                weight_quantize("out", 1)
            if y_pair is not None:
                second_stage(y_pair, 0)
            if i > 0:
                h_quantize(i - 1)
            if i % 2 == 0 and i // 2 + 1 < len(CHUNKS):
                x_quantize(i // 2 + 1)
            first_stage("car", i + 1, 1)
            first_stage("car", i + 1, 0)
            if y_pair is not None:
                second_stage(y_pair, 1)
            if done_pair is not None:
                material_out(done_pair)
            if slopes_due and square_engine == "scalar":
                slope_square(done_pair - 1, done_pair + 1, "scalar")
            if i == 0:
                weight_interleave("out", 0, 1, "scalar")
            window_exp(i + 1)
            if blend_pair is not None:
                x_blend(blend_pair)
            if i == 1:
                weight_interleave("out", 1, 0, "scalar")
                weight_interleave("out", 1, 1, "vector")
            if next_pair is not None:
                x_coarse(2 * next_pair + 1)
            if slopes_due and square_engine == "vector":
                slope_square(done_pair - 1, done_pair + 1, "vector")
            h_product(i, 3)
            if slopes_due:
                slope_sum(done_pair - 1, done_pair + 1)

            psum_columns = (2 * OUT if y_pair is not None else 0) + (3 if i + 1 < last else SLOTS) * texels[i + 1]
            share = int((psum_columns - GPSIMD_LEAD) * GPSIMD_RATE) // SHARE_STEP * SHARE_STEP
            gpsimd_share[i] = min(share, texels[i])
            h_interleave(i, "gpsimd", 0, gpsimd_share[i])
            if i + 2 <= last:
                first_stage("win", i + 2, 1)
                first_stage("win", i + 2, 0)
                window_square(i + 2, 0)
                window_square(i + 2, 1)
            if y_pair is not None:
                y_bias(y_pair, 0, OUT)
        assert gpsimd_share[last - 1] == texels[last - 1]

        final = PAIRS - 1
        first_stage("car", last, 3)
        first_stage("car", last, 2)
        material_out(final - 1)
        for t in range(SLOTS):
            h_product(last, t)
        h_quantize(last - 1)
        second_stage(final, 0)
        h_interleave(last, "vector", 0, texels[last])
        inverse_root(0, 2)
        inverse_root(2, 4)
        slope_square(final - 1, final, "scalar")
        h_quantize(last)
        second_stage(final, 1)
        normal_out(0, 2)
        slope_sum(final - 1, final)
        inverse_root(4, final)
        y_bias(final, PLANES, OUT)
        slope_square(final, PAIRS, "scalar")
        normal_out(2, 4)
        slope_sum(final, PAIRS)
        inverse_root(final, PAIRS)
        y_bias(final, 0, PLANES)
        normal_out(4, 6)
        normal_out(6, PAIRS)
        material_out(final, 0, 1)
        material_out(final, 1, 2)
